import numpy as np, ml_dtypes
CORES = [2,6,10,14,18,22,26,30]
N = 8
import mx_ref
BF = ml_dtypes.bfloat16
def gentries(a):
    return np.ascontiguousarray(a.reshape(8, 16, -1).transpose(0, 2, 1)).reshape(8, -1)
def gtable(e):
    e = np.asarray(e); return np.ascontiguousarray(e.reshape(8, -1, 16).transpose(0, 2, 1)).reshape(128, -1).astype(np.int32)
def gcols(t, e):
    v = np.concatenate([t.reshape(8, 16, -1, 4), np.zeros((8, 16, 1, 4), BF)], axis=2)
    return np.ascontiguousarray(np.stack([v[g][:, e[g]] for g in range(8)])).reshape(128, -1)
def tile(rs):
    return np.stack(rs, axis=2).reshape(128, -1).astype(BF)
def pick(q, e):
    c = np.concatenate([q[0].reshape(128, -1, 4), np.zeros((128, 1, 4), np.uint8)], axis=1); s = np.concatenate([q[1], np.ones((16, 1), np.uint8)], axis=1)
    return (np.ascontiguousarray(c[:, e].reshape(128, -1)), np.ascontiguousarray(s[:, e]))
def join(*qs):
    return (np.concatenate([q[0] for q in qs], axis=1), np.concatenate([q[1] for q in qs], axis=1))
def put(q, e, v):
    c, s = q[0].reshape(128, -1, 4).copy(), q[1].copy(); c[:, e] = v[0].reshape(128, -1, 4); s[:, e] = v[1]
    return (c.reshape(128, -1), s)
def pk(c, s):
    return (np.ascontiguousarray(c), mx_ref.live(s))
def emit(q):
    return q[0], q[1]
def packed(v, rng):
    q = [mx_ref.quantize(np.ascontiguousarray(v[r])) for r in range(N)]
    return np.stack([a for a, b in q]), np.stack([mx_ref.plane(b, rng) for a, b in q])
def values_of_codes():
    e, c = np.zeros((128, 128, 4), np.float32), np.zeros((128, 2, 4), np.uint8)
    e[np.arange(128), np.arange(128), 0] = 1
    c[:127, :, 0] = np.arange(256).reshape(2, 128).T[:127]
    return mx_ref.matmul(mx_ref.quantize(e.reshape(128, 512).astype(BF)), (c.reshape(128, 8), np.full((16, 2), 127, np.uint8))).T.reshape(-1).astype(np.float64)
CODE_VALUE, SCALE_VALUE = values_of_codes(), 2.0 ** (np.arange(256) - 127.0)
def decode(q):
    return (CODE_VALUE[q[0]].reshape(16, 8, -1, 4) * SCALE_VALUE[q[1]][:, None, :, None] + 0.0).reshape(128, -1).astype(np.float32)
def f(rng, *shape):
    return mx_ref.flush((rng.standard_normal(shape, dtype=np.float32) * np.exp2(rng.integers(-2, 3, shape[:-1] + (1,)))).astype(BF))
def wide(rng, *shape, cols=0):
    v = rng.standard_normal(shape, dtype=np.float32) * np.exp2(rng.integers(-12, 13, shape)).astype(np.float32)
    if cols: v *= np.repeat(np.exp2(rng.integers(-cols, cols + 1, shape[:-2] + (1, shape[-1] // 4))) * (rng.random(shape[:-2] + (1, shape[-1] // 4)) > 0.0625), 4, axis=-1).astype(np.float32)
    return mx_ref.flush(v.astype(BF))
C = 256
STEP = [1, 2, 4]
HOPS = 128
def numbers_of(rng):
    return {"x": np.array(f(rng, N, 128, 4 * C)), "u": np.array(f(rng, N, 128, 512)), "v": np.array(f(rng, N, 128, 512))}
def orders(rng):
    e = np.tile(np.arange(C), (N, 8, 1))
    k, a, t = rng.permuted(e, axis=2), rng.permuted(e, axis=2)[:, :, 16:], e.copy()
    np.put_along_axis(t, a[:, :, 0::2], a[:, :, 1::2], axis=2)
    np.put_along_axis(t, a[:, :, 1::2], a[:, :, 0::2], axis=2)
    return k, t
def stored(k, t):
    return {"nx": np.stack([gtable(k[r]) for r in range(N)]), "mt": np.stack([gtable(t[r]) for r in range(N)])}
def layers(rng, still=[]):
    w = np.array(f(rng, N, 128, 2048)).reshape(N, 8, 16, 4, 8, 16, 4)
    for i in still:
        w[:, :, i] = 0
        w[:, :, :, :, :, i] = 0
    return w
def weights(rng, w):
    c, p = packed(np.ascontiguousarray(w).reshape(N, 128, 2048), rng)
    return {"wc": c, "ws": p}
def setup_inputs(rng):
    return {**numbers_of(rng), **stored(*orders(rng)), **weights(rng, layers(rng))}
def setup_inputs_ties(rng):
    d = numbers_of(rng)
    k, t = orders(rng)
    o = rng.permutation(N) % 4
    n = rng.integers(0, 4, (N, 8, C))
    c = np.ones((N, 8), np.float32)
    for r in range(N):
        c[r] = rng.permutation(8) % 2 * 2.0 - 1.0
        for g in range(8):
            if o[r] < 2:
                e = rng.permutation(C)
                a = np.arange(C) + 1 if c[r, g] < 0 else C - np.arange(C)
                n[r, g, e] = a if o[r] == 0 else (a + 1) // 2
                k[r, g, e] = np.roll(e, -1)
            if o[r] == 3: n[r, g] = rng.integers(0, 2, C) if g % 2 else 1
        if o[r] < 2: t[r, rng.permutation(8)[:4]] = np.arange(C)
    digits = (n[..., None] & (1 << np.arange(12))).reshape(N, 8, C, 3, 4)
    x = d["x"].reshape(N, 8, 16, C, 4)
    x[:, :, 8:] = 0
    x[:, :, 8:11] = digits.transpose(0, 1, 3, 2, 4).astype(np.float32).astype(BF)
    u = d["u"].reshape(N, 128, 128, 4)
    u[:, :, ::16] = 0
    for g in range(8): u[:, 16 * g + 8:16 * g + 11, 16 * g] = c[:, g].astype(BF)[:, None, None]
    w = layers(rng)
    w[:, :, :, :, :, 8:] = 0
    return {"x": x.reshape(N, 128, 4 * C), "u": u.reshape(N, 128, 512), "v": d["v"], **stored(k, t), **weights(rng, w)}
def setup_inputs_near(rng):
    d = numbers_of(rng)
    x = d["x"].astype(np.float32).reshape(N, 8, 16, C, 4)
    x[:, :, :2] = 0
    x[:, :, 8:] = 0
    u = d["u"].reshape(N, 128, 128, 4)
    u[:, :, ::16] = 0
    w = layers(rng, [0, 1, 8, 9, 10, 11, 12, 13, 14, 15])
    o = (np.arange(N) + rng.integers(N)) % 4
    for r in range(N):
        c = rng.choice([-1.0, 1.0], (8, 1))
        s = rng.integers(0, 16, (8, C))
        digits = ((s[:, :, None] >> np.arange(4)) & 1) * np.exp2(np.arange(4) - 23.0)
        if o[r] < 2:
            x[r, :, 0, :, 0] = c
            x[r, :, 8] = digits
            x[r, :, 11, :, 0] = 2.0 ** -10
        else:
            x[r, :, :8] = 0
            x[r, :, 13, :, 0] = 2.0 ** -30
            x[r, :, 1, :, 0] = rng.choice([-1.0, 1.0], (8, C)) * 2.0 ** -30
            w[r] = 0
            for g in range(8): w[r, g, 1, 0, g, 12, 0] = 2.0 ** -8
        if o[r] == 2: x[r, :, 8] = digits * rng.choice([-1.0, 1.0], (8, C, 1))
        if o[r] == 3:
            x[r, :, 8, :, 0] = np.where(s < 8, 1.25, 0.0) * 2.0 ** -30 * c
            x[r, :, 9, :, 0] = np.where(s < 8, 0.0, 1.125) * 2.0 ** -30 * c
            for g in rng.permutation(8)[:4]:
                e = rng.choice([-1.0, 1.0], C) * 2.0 ** -30
                x[r, g, 8, :, 0] = 1.25 * e
                x[r, g, 9, :, 0] = -1.125 * e
        at = [0, C - 1, int(rng.integers(C)), int(rng.integers(C))]
        for g, j in zip(rng.permutation(8)[:4], at): x[r, g, 0, j, 0] = 2.0 ** 29 * rng.choice([-1.0, 1.0])
        k = 1.0 if o[r] == 0 else 2.0 ** -30
        for h in range(0, 128, 16):
            u[r, h, h, 0] = k if o[r] < 2 else 1.0
            if o[r] < 2: u[r, h + 11, h, 0] = k
            if o[r] < 3: u[r, h + 8, h] = k
            else:
                u[r, h + 8, h, 0] = k
                u[r, h + 9, h, 0] = 1.125 * k
                u[r, h + 12, h, 0] = k
    return {"x": x.reshape(N, 128, 4 * C).astype(BF), "u": u.reshape(N, 128, 512), "v": d["v"], **stored(*orders(rng)), **weights(rng, w)}
def setup_inputs_odd(rng):
    d = numbers_of(rng)
    w = layers(rng, [0, 8])
    x = (1.0 + (2 * rng.integers(0, 64, (N, 16, 8, C, 4)) + 1) * 2.0 ** -7) * np.exp2(-rng.integers(0, 7, (N, 16, 8, C, 4)).astype(np.float64)) * rng.choice([-1.0, 1.0], (N, 16, 8, C, 4))
    x[:, 0::2, 0, :, 0] = 1.96875 * 2.0 ** 8 * rng.choice([-1.0, 1.0], (8, 1))
    x[:, 1::2, 0, :, 0] = rng.choice([1.96875 * 2.0 ** 8, 8.0], (N, 8, C)) * rng.choice([-1.0, 1.0], (N, 8, C))
    for g in range(8): w[:, g, 0, 0, g, 0, 0] = -0.5
    u = d["u"].reshape(N, 16, 8, 128, 4)
    u[:, :, 0, ::16] = 0
    for r in rng.permutation(N)[:N // 2]:
        for i, g in enumerate(rng.permutation(8)[:4]):
            x[r, 2 * g, 1, :, 0] = (8 + rng.integers(0, 2, C)) * 2.0 ** (i - 8)
            u[r, :, :, 16 * g] = 0
            u[r, 2 * g, 1, 16 * g, 0] = 1.0
            w[r, :, :, 0, g, 1] = 0
    return {"x": x.astype(np.float32).reshape(N, 128, 4 * C).astype(BF), "u": u.reshape(N, 128, 512), "v": d["v"], **stored(*orders(rng)), **weights(rng, w)}
def setup_inputs_ends(rng):
    d = numbers_of(rng)
    k, t = orders(rng)
    o, e, m = rng.permutation(N) % 4, rng.permutation(N) % 4, rng.permutation(N) % 4
    for r in range(N):
        s = (r - STEP[-1]) % N
        if o[r] == 3 and o[s] == 2:
            a = rng.choice([n for n in range(N) if o[n] < 2 and o[(n + STEP[-1]) % N] != 3])
            o[s] = o[a]
            o[a] = 2
    i = np.arange(C)
    k[e == 0] = i
    k[e == 1] = (i + 1) % C
    k[e == 2] = C - 1 - i
    k[e == 3] = (i - 1) % C
    t[m == 0] = i
    t[m == 1] = C - 1 - i
    t[m == 2] = i ^ 1
    x = np.zeros((N, 8, 16, C, 4))
    u = d["u"].astype(np.float32).reshape(N, 128, 128, 4)
    v = d["v"].astype(np.float32)
    w = np.zeros((N, 128, 4, 128, 4), np.float32)
    j = np.arange(128)
    for r in range(N):
        h = rng.permutation(8)
        c = np.where(h < 2, 0.0, h % 2 * 2.0 - 1.0)[None, :, None]
        low = -(0.7 + 0.1 * rng.random((8, 16, C, 4))) * 2.0 ** 30
        if o[r] == 0: x[r] = low
        if o[r] == 1: x[r] = low * rng.choice([-1.0, 1.0], (C, 1))
        if o[r] == 2: x[r] = -(1.0 + 0.125 * rng.integers(0, 8, (8, 16, C, 4))) * 2.0 ** -30
        if o[r] == 3: x[r] = d["x"][r].astype(np.float32).reshape(8, 16, C, 4)[:, :, :1]
        if o[r] < 2:
            u[r, :, ::16] = c * (0.9 + 0.1 * rng.random((128, 8, 4))) * 2.0 ** 30
            v[r] = rng.choice([-1.0, 1.0], (128, 512)) * (0.9 + 0.1 * rng.random((128, 512))) * 2.0 ** 30
        if o[r] == 2:
            u[r, :, ::16] = c * (1.0 + 0.125 * rng.integers(0, 8, (128, 8, 4))) * 2.0 ** -30
            v[r] = rng.choice([-1.0, 1.0], (128, 512)) * (1.0 + 0.125 * rng.integers(0, 8, (128, 512))) * 2.0 ** -30
        if o[r] == 3: u[r, :, ::16] *= np.abs(c).astype(np.float32)
        a = np.array([2.0, 2.0 ** -8, -0.25])[rng.permutation(8) % 3][j // 16]
        if o[r] == 2: a = np.zeros(128)
        a[120:] = 256.0
        for b in range(4): w[r, j, b, j, b] = a
    x[:, 7, 8:] = -2.0 ** -30
    return {"x": x.astype(np.float32).reshape(N, 128, 4 * C).astype(BF), "u": u.reshape(N, 128, 512).astype(BF), "v": v.astype(BF), **stored(k, t), **weights(rng, w.astype(BF))}
def setup_inputs_spread(rng):
    d = setup_inputs(rng)
    d["x"] = wide(rng, N, 128, 4 * C, cols=6)
    return d
def check_inputs(d):
    b = []
    for k in ("x", "u", "v"):
        a = np.abs(d[k].astype(np.float32))
        if not (np.isfinite(a).all() and ((a == 0) | (a >= 2.0 ** -30) & (a <= 2.0 ** 30)).all()): b.append("a value of " + k)
    none, least, most = [emit(mx_ref.quantize(np.full((128, 16), k, np.float32).astype(BF)))[1][0, 0] for k in (0.0, 2.0 ** -8, 2.0 ** 8)]
    for r in range(N):
        k, t = gentries(d["nx"][r]), gentries(d["mt"][r])
        if not (np.sort(k, axis=1) == np.arange(C)).all(): b.append("nx: not every column once")
        if not (((t >= 0) & (t < C)).all() and (np.take_along_axis(t, np.clip(t, 0, C - 1), axis=1) == np.arange(C)).all()): b.append("mt: not each other's")
        if ((d["wc"][r] == 0x7F) | (d["wc"][r] == 0xFF)).any(): b.append("wc: a code that is no number")
        s = mx_ref.live(d["ws"][r])
        if ((s != none) & ((s < least) | (s > most))).any(): b.append("ws: a scale out of range")
        if (((d["wc"][r].reshape(16, 8, 512, 4) & 0x7F) != 0) & (s == none)[:, None, :, None]).any(): b.append("wc: a code other than zero under the scale of zeros")
    return b
def at(a, e):
    return np.take_along_axis(a, e, axis=1)
def search(s, follow):
    b = np.tile(np.arange(C), (8, 1))
    p, left = b.copy(), np.ones((8, C), bool)
    for hop in range(1, HOPS + 1):
        to = at(follow, p)
        larger = left & (at(s, to) > s)
        b = np.where(larger, to, b)
        left = left & ~larger
        if hop < HOPS: p = np.where(left, to, p)
    return b, p
def layer(w, q):
    return tile([mx_ref.matmul(pick(w, np.arange(128 * k, 128 * k + 128)), q) * np.float32(0.03125) for k in range(4)])
def reference(x, u, v, nx, mt, wc, ws):
    qu = [mx_ref.quantize(u[r]) for r in range(N)]
    lay = [pk(wc[r], ws[r]) for r in range(N)]
    follow, mate = [gentries(nx[r]) for r in range(N)], [gentries(mt[r]) for r in range(N)]
    now = [x[r] for r in range(N)]
    for step in STEP:
        t, z, first = [], [], []
        for r in range(N):
            q = mx_ref.quantize(now[r])
            s = mx_ref.matmul(qu[r], q)[::16] + np.float32(0.0)
            b, p = search(s, follow[r])
            t.append(decode(q))
            c = t[r].astype(BF)
            z.append(mx_ref.quantize(((gcols(c, b).astype(np.float32) + gcols(c, p).astype(np.float32)) * np.float32(0.5)).astype(BF)))
            first.append(b)
            e = at(s, b)
            swap = at(e, np.minimum(mate[r], np.arange(C))) > at(e, np.maximum(mate[r], np.arange(C)))
            follow[r] = np.where(swap, at(follow[r], mate[r]), follow[r])
        now = [(t[r] + gcols(layer(lay[r], z[(r - step) % N]), first[r]).astype(np.float32)).astype(BF) for r in range(N)]
    y, nf = np.zeros((N, 128, C), np.float32), np.zeros((N, 8, C), np.float32)
    oc, osc = np.zeros((N, 128, 4 * C), np.uint8), np.zeros((N, 16, C), np.uint8)
    for r in range(N):
        q = mx_ref.quantize(now[r])
        y[r] = mx_ref.matmul(mx_ref.quantize(v[r]), q)
        nf[r] = follow[r]
        oc[r], osc[r] = emit(q)
    return {"y": y, "nf": nf, "oc": oc, "osc": osc}

@@ -1,0 +1,359 @@
+from concourse.mybir import dt, AluOpType as A, ActivationFunctionType as F
+
+STEP = [1, 2, 4]
+C = 256
+R3 = 3
+CODE = "float8_e4m3fn_x4"
+SCRATCH = {
+    "ps": ("psum", [128, 4096], "float32"),
+    "ut": ("sbuf", [128, 512], "bfloat16"), "vt": ("sbuf", [128, 512], "bfloat16"),
+    "qu0": ("sbuf", [128, 128], CODE), "su0": ("sbuf", [128, 128], "uint8"),
+    "qu": ("sbuf", [128, 128], CODE), "su": ("sbuf", [128, 128], "uint8"),
+    "qv": ("sbuf", [128, 128], CODE), "sv": ("sbuf", [128, 128], "uint8"),
+    "wq": ("sbuf", [128, 512], CODE), "wp": ("sbuf", [128, 512], "uint8"),
+    "ones": ("sbuf", [128, 520], "bfloat16"), "et": ("sbuf", [128, 520], "bfloat16"),
+    "qe": ("sbuf", [128, 512], CODE), "se": ("sbuf", [128, 512], "uint8"),
+    "nxi": ("sbuf", [128, 16], "int32"), "mti": ("sbuf", [128, 16], "int32"),
+    "tj": ("sbuf", [128, 256], "float32"), "ii": ("sbuf", [128, 256], "float32"),
+    "idn": ("sbuf", [128, 256], "bfloat16"),
+    "pi": ("sbuf", [128, 8], "int32"), "qf": ("sbuf", [128, 8], "float32"), "inv": ("sbuf", [128, 8], "float32"),
+    "k16": ("sbuf", [128, 16], "float32"), "cw": ("sbuf", [128, 16], "float32"),
+    "d1": ("sbuf", [128, 256], "float32"), "d2": ("sbuf", [128, 256], "float32"),
+    "mka": ("sbuf", [128, 256], "float32"),
+    "mkf": ("sbuf", [128, 256], "float32"),
+    "dl": ("sbuf", [128, 256], "bfloat16"), "dsum": ("sbuf", [128, 256], "bfloat16"),
+    "lid": ("sbuf", [128, 16], "uint16"), "lu": ("sbuf", [128, 8], "uint16"), "lui": ("sbuf", [128, 8], "int32"),
+    "lm": ("sbuf", [128, 16], "uint16"), "lmin": ("sbuf", [128, 16], "uint16"), "lmax": ("sbuf", [128, 16], "uint16"),
+    "mf": ("sbuf", [128, 16], "float32"), "mmin": ("sbuf", [128, 16], "float32"), "mmax": ("sbuf", [128, 16], "float32"),
+    "sw": ("sbuf", [128, 256], "float32"), "s1": ("sbuf", [128, 256], "float32"), "s2": ("sbuf", [128, 256], "float32"),
+    "n6": ("sbuf", [128, 256], "bfloat16"), "nsc": ("sbuf", [128, 256], "bfloat16"),
+    "fm": ("sbuf", [128, 256], "bfloat16"), "fms": ("sbuf", [128, 256], "bfloat16"), "fmw": ("sbuf", [128, 16], "float32"),
+    "dfm": ("sbuf", [128, 16], "float32"), "tt": ("sbuf", [128, 16], "float32"),
+    "sb": ("sbuf", [128, 256], "float32"), "xm": ("sbuf", [128, 256], "float32"),
+    "swb": ("sbuf", [128, 256], "bfloat16"), "sws": ("sbuf", [128, 256], "bfloat16"),
+    "nff": ("sbuf", [128, 256], "float32"), "yt": ("sbuf", [128, 256], "float32"),
+    "fa": ("sbuf", [128, 1024], "bfloat16"), "fo": ("sbuf", [128, 1024], "bfloat16"),
+    "zg": ("sbuf", [128, 1024], "bfloat16"), "z": ("sbuf", [128, 1024], "bfloat16"), "hh": ("sbuf", [128, 1024], "bfloat16"),
+    "qz": ("sbuf", [128, 256], CODE), "sz": ("sbuf", [128, 256], "uint8"),
+    "vbz": ("sbuf", [128, 512], "bfloat16"),
+}
+for _i in range(2):
+    SCRATCH["mc%d" % _i] = ("sbuf", [128, 256], "float32")
+    for _n in ("cb", "vb", "rb"):
+        SCRATCH["%s%d" % (_n, _i)] = ("sbuf", [128, 512], "bfloat16")
+    SCRATCH["nb%d" % _i] = ("sbuf", [128, 256], "bfloat16")
+    SCRATCH["lw%d" % _i] = ("sbuf", [128, 16], "uint16")
+    SCRATCH["fw%d" % _i] = ("sbuf", [128, 16], "float32")
+for _i in range(4):
+    SCRATCH["x%d" % _i] = ("sbuf", [128, 1024], "bfloat16")
+    SCRATCH["qx%d" % _i] = ("sbuf", [128, 256], CODE)
+    SCRATCH["sx%d" % _i] = ("sbuf", [128, 256], "uint8")
+for _i in range(3):
+    SCRATCH["lq%d" % _i] = ("sbuf", [128, 256], CODE)
+    SCRATCH["ls%d" % _i] = ("sbuf", [128, 256], "uint8")
+    for _n in ("lp", "lb", "zp", "zb"):
+        SCRATCH["%s%d" % (_n, _i)] = ("sbuf", [128, 16], "uint16")
+for _i in range(7):
+    SCRATCH["m%d" % _i] = ("sbuf", [128, 256], "float32")
+for _i in range(6):
+    SCRATCH["n%d" % _i] = ("sbuf", [128, 256], "bfloat16")
+    SCRATCH["l%d" % _i] = ("sbuf", [128, 16], "uint16")
+DMAS = ["dx", "dnx", "dmt", "du", "dwc", "dws", "dv", "doc", "dos0", "dos1", "dos2", "dos3", "dy", "dnf"]
+SEMAPHORES = ["cv", "cs", "ct", "cg", "sent"] + DMAS + ["%s%d" % (n, i) for n in ("arq", "arp", "arb") for i in range(3)]
+BIG = 1.0e29
+
+
+def make_issue(g, T):
+    queue = {"v": g.vector, "s": g.scalar, "t": g.tensor, "g": g, "y": g.sync}
+    known = {e: {} for e in queue}
+    count, clock, writer, readers = {}, {}, {}, {}
+
+    def learn(e, ev):
+        sem, val = ev
+        for s, n in list(clock.get(ev, {}).items()) + [(sem, val)]:
+            if known[e].get(s, 0) < n:
+                known[e][s] = n
+
+    def need(e, evs):
+        todo = sorted(set(evs), key=lambda ev: -len(clock.get(ev, {})))
+        best = {}
+        for sem, val in todo:
+            if known[e].get(sem, 0) < val:
+                best[sem] = max(best.get(sem, 0), val)
+        evs = [(sem, val) for sem, val in best.items()]
+        keep = []
+        for ev in evs:
+            if not any(o != ev and clock.get(o, {}).get(ev[0], 0) >= ev[1] for o in evs):
+                keep.append(ev)
+        for ev in keep:
+            queue[e].wait_ge(T.sem[ev[0]], ev[1])
+        for ev in evs:
+            learn(e, ev)
+
+    def wait_for(e, reads=(), writes=()):
+        evs = []
+        for k in reads:
+            if k in writer:
+                evs.append(writer[k][0])
+            if k.startswith("ps"):
+                evs += [ev for ev, o in readers.get(k, []) if o != e]
+        for k in writes:
+            if k in writer:
+                evs.append(writer[k][0])
+            evs += [ev for ev, o in readers.get(k, [])]
+        need(e, evs)
+
+    def op(e, call, reads=(), writes=(), sem=None, inc=1):
+        wait_for(e, reads, writes)
+        sem = sem or "c" + e
+        call(queue[e]).then_inc(T.sem[sem], inc)
+        count[sem] = count.get(sem, 0) + inc
+        ev = (sem, count[sem])
+        clock[ev] = dict(known[e])
+        for k in reads:
+            readers.setdefault(k, []).append((ev, e))
+        for k in writes:
+            writer[k] = (ev, e)
+            readers[k] = []
+
+    def lands(key, sem, val):
+        writer[key] = ((sem, val), "remote")
+        readers[key] = []
+
+    return op, wait_for, lands, count
+
+
+def rank_program(g, core, T, topo):
+    rank = T.rank_of(core)
+    if rank is None:
+        return
+    op, wait_for, lands, count = make_issue(g, T)
+    cores = T.cores
+    U8, U32 = dt.uint8, dt.uint32
+    sent = [0]
+
+    def few(src, dst):
+        return topo.engines(src, dst)[:8]
+
+    def send(dst, out, src, sem, reads):
+        wait_for("g", reads)
+        rid, pid = topo.addr(dst)[:2]
+        e = few(core, dst)
+        g.remote_dma(out, src, T.sem[sem], T.sem.sent, pid, rid, sum(1 << k for k in e))
+        sent[0] += len(e)
+
+    def V(call, reads, writes):
+        op("v", call, reads, writes)
+
+    def S(call, reads, writes):
+        op("s", call, reads, writes)
+
+    def bank(b):
+        return T.ps[:, 512 * b:512 * b + C]
+
+    def mm(b, stat, stats, c0, mov, movs):
+        op("t", lambda q: q.matmul_mx(bank(b), T[stat][:, c0:c0 + 128], T[stats][:, c0:c0 + 128], T[mov][:, 0:C], T[movs][:, 0:C], True, True),
+           [stat, mov], ["ps%d" % b])
+
+    def quant(q, s, tile, keys=None):
+        V(lambda v: v.quantize_mx(T[q][:, :], T[s][:, :], T[tile][:, :]), keys or [tile], [q])
+
+    def pick(win, lst, a=0, n=C):
+        return T[win][:, a:a + n].indirect(T[lst][:, 0:16])
+
+    op("y", lambda q: q.dma_start(T.nxi[:], T.nx[:]), [], ["nxi"], "dnx", 16)
+    op("s", lambda q: q.dma_start(T.x0[:], T.x[:]), [], ["x0"], "dx", 16)
+    op("y", lambda q: q.dma_start(T.ut[:], T.u[:]), [], ["ut"], "du", 16)
+    op("y", lambda q: q.dma_start(T.mti[:], T.mt[:]), [], ["mti"], "dmt", 16)
+    op("y", lambda q: q.dma_start(T.wq[:, 0:512].bitcast(U8), T.wc[:]), [], ["wq"], "dwc", 16)
+    op("y", lambda q: q.dma_start(T.wp[:, 0:512], T.ws[:]), [], ["wp"], "dws", 16)
+    op("y", lambda q: q.dma_start(T.vt[:], T.v[:]), [], ["vt"], "dv", 16)
+
+    op("g", lambda q: q.iota(T.pi[:, 0:1], [[0, 1]], 0, 1), [], ["pi"])
+    op("g", lambda q: q.iota(T.tj[:], [[0, 16], [1, 16]], 0, 0, allow_small_or_imprecise_dtypes=True), [], ["tj"])
+    op("g", lambda q: q.iota(T.ii[:], [[1, 256]], 1, 0, allow_small_or_imprecise_dtypes=True), [], ["ii"])
+    op("g", lambda q: q.iota(T.k16[:], [[16, 16]], 0, 0, allow_small_or_imprecise_dtypes=True), [], ["k16"])
+    op("g", lambda q: q.iota(T.lui[:], [[16, 8]], 0, 0), [], ["lui"])
+    V(lambda v: v.memset(T.ones[:], 1.0), [], ["ones"])
+    op("g", lambda q: q.affine_select(T.et[:], T.ones[:], [[-1, 520]], A.is_equal, 0.0, 3, 4), ["ones"], ["et"])
+    for b in ("cb0", "cb1"):
+        V(lambda v: v.memset(T[b][:], 1.0), [], [b])
+    for b in ("vbz", "vb0", "vb1"):
+        V(lambda v: v.memset(T[b][:], -1.0), [], [b, b + ".0"])
+    for b in ("cb0", "cb1"):
+        V(lambda v: v.memset(T[b][:, 0:512:32], 0.0), [b], [b])
+    V(lambda v: v.tensor_scalar(T.pi[:, 4:5], T.pi[:, 0:1], 15, None, A.bitwise_and), ["pi"], ["qi"])
+    V(lambda v: v.tensor_copy(T.qf[:, 0:1], T.pi[:, 4:5]), ["qi"], ["qf"])
+    V(lambda v: v.tensor_scalar(T.inv[:, 4:5], T.qf[:, 0:1], 15.0, 511.5, A.is_equal, A.mult), ["qf"], ["inv5"])
+    V(lambda v: v.tensor_scalar(T.d1[:], T.tj[:], T.qf[:, 0:1], None, A.subtract), ["tj", "qf"], ["e"])
+    V(lambda v: v.tensor_scalar(T.idn[:], T.ii[:], 1.0 / 512, None, A.mult), ["ii"], ["idn"])
+    V(lambda v: v.tensor_scalar(T.inv[:, 0:1], T.inv[:, 4:5], 0.5, None, A.add), ["inv5"], ["inv"])
+    V(lambda v: v.tensor_scalar(T.d2[:], T.d1[:], 0.0, None, A.not_equal), ["e"], ["d2"])
+    V(lambda v: v.tensor_scalar(T.cw[:], T.k16[:], T.qf[:, 0:1], None, A.add), ["k16", "qf"], ["cw"])
+    V(lambda v: v.tensor_scalar(T.ii[:], T.d1[:], 1.0, 1023.0, A.is_equal, A.mult), ["e"], ["ii"])
+    V(lambda v: v.tensor_copy(T.lid[:], T.cw[:]), ["cw"], ["lid"])
+    V(lambda v: v.tensor_tensor(T.dl[:], T.ii[:], T.d2[:], A.add), ["ii", "d2"], ["dl"])
+    V(lambda v: v.tensor_copy(T.l0[:], T.nxi[:]), ["nxi"], ["l0"])
+    S(lambda s: s.activation(T.n0[:], pick("idn", "l0"), F.Copy), ["idn", "l0"], ["n0"])
+    S(lambda s: s.activation(T.n1[:], pick("n0", "l0"), F.Copy), ["n0", "l0"], ["n1"])
+    V(lambda v: v.tensor_copy(T.fw0[:], T.nxi[:]), ["nxi"], ["fw0"])
+    V(lambda v: v.tensor_copy(T.lu[:], T.lui[:]), ["lui"], ["lu"])
+    quant("qu0", "su0", "ut")
+    V(lambda v: v.tensor_copy(T.qu[:, 0:128].bitcast(U32), T.qu0[:, 0:128].bitcast(U32).indirect(T.lu[:, 0:8])), ["qu0", "lu"], ["qu"])
+    V(lambda v: v.tensor_copy(T.su[:, 0:128], T.su0[:, 0:128].indirect(T.lu[:, 0:8])), ["qu0", "lu"], ["su"])
+    quant("qx0", "sx0", "x0")
+
+    def level(k):
+        V(lambda v: v.tensor_tensor_scan(T.nsc[:], T.dl[:], T["n%d" % k][:], 0.0, A.mult, A.max), ["dl", "n%d" % k], ["nsc"])
+        V(lambda v: v.tensor_scalar(T["l%d" % k][:], T.nsc[:, 15:256:16], T.inv[:, 0:1], 1.0, A.mult, A.subtract), ["nsc", "inv"], ["l%d" % k])
+
+    def hop(k):
+        out = T.n6[:] if k == 6 else T["n%d" % k][:]
+        S(lambda s: s.activation(out, pick("n%d" % (k - 1), "l%d" % (k - 1)), F.Copy), ["n%d" % (k - 1), "l%d" % (k - 1)], ["n%d" % k])
+
+    def mates_pick():
+        S(lambda s: s.activation(T.fm[:], pick("n0", "lm"), F.Copy), ["n0", "lm"], ["fm"])
+
+    def mates_list(fw):
+        V(lambda v: v.tensor_tensor_scan(T.fms[:], T.dl[:], T.fm[:], 0.0, A.mult, A.max), ["dl", "fm"], ["fms"])
+        V(lambda v: v.tensor_scalar(T.fmw[:], T.fms[:, 15:256:16], T.inv[:, 0:1], 1.0, A.mult, A.subtract), ["fms", "inv"], ["fmw"])
+        V(lambda v: v.tensor_tensor(T.dfm[:], T.fmw[:], T[fw][:], A.subtract), ["fmw", fw], ["dfm"])
+
+    def up(k):
+        if k == 0:
+            V(lambda v: v.tensor_copy(T.m0[:], pick("sw", "l0")), ["sw", "l0"], ["m0"])
+            return
+        win, l, other = ("sw", "l1", "m0") if k == 1 else ("m%d" % (k - 1), "l%d" % (k - 1), "mc%d" % (k % 2))
+        if k > 1:
+            S(lambda s: s.activation(T[other][:], T[win][:], F.Copy), [win], [other])
+        V(lambda v: v.tensor_tensor(T["m%d" % k][:], pick(win, l), T[other][:], A.max), [win, l, other], ["m%d" % k])
+
+    def unpack(b, pb, out, half):
+        S(lambda s: s.activation(T[out][:, C * b:C * b + C], bank(pb), F.Copy, scale=0.5 if half else 1.0), ["ps%d" % pb], ["%s.%d" % (out, b)])
+
+    for r in range(R3):
+        d = STEP[r]
+        to = cores[(rank + d) % len(cores)]
+        qx, sx, fw, fwn = "qx%d" % r, "sx%d" % r, "fw%d" % (r % 2), "fw%d" % ((r + 1) % 2)
+        lq, ls, zp, zb, lp, lb = ["%s%d" % (n, r) for n in ("lq", "ls", "zp", "zb", "lp", "lb")]
+        eng = len(few(cores[(rank - d) % len(cores)], core))
+        lands(lq, "arq%d" % r, 2 * eng)
+        lands(zp, "arp%d" % r, eng)
+        lands(zb, "arb%d" % r, eng)
+        send(to, T[lq][:, 0:C].bitcast(U8), T[qx][:, 0:C].bitcast(U8), "arq%d" % r, [qx])
+        send(to, T[ls][:, 0:C], T[sx][:, 0:C], "arq%d" % r, [qx])
+        op("t", lambda q: q.matmul_mx(bank(0), T.qu[:, 0:128], T.su[:, 0:128], T[qx][:, 0:C], T[sx][:, 0:C], True, True), ["qu", "su", qx], ["ps0"])
+        S(lambda s: s.activation(T.sw[:], bank(0), F.Copy), ["ps0"], ["sw"])
+        if r == 0:
+            level(1)
+            hop(2)
+            V(lambda v: v.tensor_scalar(T.mka[:], T.d2[:], -2.0 * BIG, BIG, A.mult, A.add), ["d2"], ["mka"])
+            V(lambda v: v.tensor_scalar(T.mkf[:], T.d2[:], 2.0 * BIG, -BIG, A.mult, A.add), ["d2"], ["mkf"])
+        level(2)
+        up(0)
+        hop(3)
+        if r == 0:
+            for b in range(4):
+                V(lambda v: v.quantize_mx(T.qe[:, 128 * b:128 * b + 128], T.se[:, 128 * b:128 * b + 128], T.et[:, 3 - b:515 - b]), ["et"], ["qe"])
+        V(lambda v: v.tensor_tensor(T.s1[:], T.ps[:, 0:256], T.mka[:], A.min), ["ps0", "mka"], ["s1"])
+        V(lambda v: v.tensor_tensor(T.s2[:], T.ps[:, 0:256], T.mkf[:], A.max), ["ps0", "mkf"], ["s2"])
+        for b in range(4):
+            mm(1 + b, "qe", "se", 128 * b, qx, sx)
+        up(1)
+        level(3)
+        up(2)
+        hop(4)
+        level(4)
+        up(3)
+        hop(5)
+        level(5)
+        up(4)
+        hop(6)
+        up(5)
+        up(6)
+        if r == 0:
+            V(lambda v: v.tensor_scalar(T.vbz[:, 0:512:32], T.cw[:], 1.0, 1.0 / 512, A.add, A.mult), ["cw"], ["vbz.0"])
+            V(lambda v: v.tensor_copy(T.mf[:], T.mti[:]), ["mti"], ["mf"])
+            V(lambda v: v.tensor_copy(T.lm[:], T.mti[:]), ["mti"], ["lm"])
+            V(lambda v: v.tensor_tensor(T.mmin[:], T.mf[:], T.cw[:], A.min), ["mf", "cw"], ["mmin"])
+            V(lambda v: v.tensor_tensor(T.mmax[:], T.mf[:], T.cw[:], A.max), ["mf", "cw"], ["mmax"])
+            V(lambda v: v.tensor_copy(T.lmin[:], T.mmin[:]), ["mmin"], ["lmin"])
+            V(lambda v: v.tensor_copy(T.lmax[:], T.mmax[:]), ["mmax"], ["lmax"])
+            V(lambda v: v.tensor_scalar(T.dsum[:], T.tj[:], 0.0, None, A.not_equal), ["tj"], ["dsum"])
+            mates_pick()
+        now = "lid"
+        for i in range(8):
+            k = 6 - i if i < 7 else 0
+            cb, nb, rb = "cb%d" % (i % 2), "nb%d" % (i % 2), "rb%d" % (i % 2)
+            vb = "vbz" if i in (0, 7) else "vb%d" % (i % 2)
+            lst = now
+            if i == 0:
+                nb = "n6"
+            else:
+                S(lambda s: s.activation(T[nb][:], pick("n%d" % k, lst), F.Copy), ["n%d" % k, lst], [nb])
+            V(lambda v: v.tensor_tensor(T[cb][:, 1:512:2], pick("m%d" % k, lst), T.s1[:] if i < 7 else T.s2[:], A.is_gt if i < 7 else A.is_le),
+              ["m%d" % k, lst, "s1" if i < 7 else "s2"], [cb])
+            if i < 2:
+                unpack(2 * i, 1 + 2 * i, "fo", False)
+                unpack(2 * i + 1, 2 + 2 * i, "fo", False)
+                for b in ((0, 1), (2, 3))[i]:
+                    mm([5, 6, 7, 1][b], "qe", "se", 128 * b, lq, ls)
+            elif i < 4:
+                for b in (2 * i - 4, 2 * i - 3):
+                    unpack(b, [5, 6, 7, 1][b], "fa", True)
+            if i == 5 and r == 0:
+                mates_list(fw)
+            V(lambda v: v.tensor_tensor_scan(T[vb][:, 1:512:2], T[nb][:], T[cb][:, 1:512:2], 0.0, A.max, A.subtract), [nb, cb], [vb])
+            V(lambda v: v.tensor_tensor_scan(T[rb][:], T[cb][:], T[vb][:], 0.0, A.mult, A.max), [cb, vb, vb + ".0"], [rb])
+            now = lp if i == 6 else lb if i == 7 else "lw%d" % (i % 2)
+            V(lambda v: v.tensor_scalar(T[now][:], T[rb][:, 31:512:32], 512.0, -1.0, A.mult, A.add), [rb], [now])
+            if i < 6:
+                nv = "vb%d" % ((i + 1) % 2)
+                V(lambda v: v.tensor_copy(T[nv][:, 0:512:32], T[rb][:, 31:512:32]), [rb], [nv + ".0"])
+            if i == 6:
+                send(to, T[zp][:], T[lp][:], "arp%d" % r, [lp])
+            if i == 7:
+                send(to, T[zb][:], T[lb][:], "arb%d" % r, [lb])
+        for t in range(4):
+            S(lambda s: s.activation(T.zg[:, C * t:C * t + C], pick("fa", zp, C * t), F.Copy), ["fa.%d" % t, zp], ["zg.%d" % t])
+        V(lambda v: v.tensor_copy(T.sb[:], pick("sw", lb)), ["sw", lb], ["sb"])
+        V(lambda v: v.tensor_tensor(T.xm[:], pick("sb", "lmax"), T.mkf[:], A.max), ["sb", "lmax", "mkf"], ["xm"])
+        V(lambda v: v.tensor_tensor(T.swb[:], pick("sb", "lmin"), T.xm[:], A.is_gt), ["sb", "lmin", "xm"], ["swb"])
+        V(lambda v: v.tensor_tensor_scan(T.sws[:], T.dsum[:], T.swb[:], 0.0, A.mult, A.add), ["dsum", "swb"], ["sws"])
+        V(lambda v: v.tensor_tensor(T.tt[:], T.sws[:, 15:256:16], T.dfm[:], A.mult), ["sws", "dfm"], ["tt"])
+        V(lambda v: v.tensor_tensor(T[fwn][:], T[fw][:], T.tt[:], A.add), [fw, "tt"], [fwn])
+        V(lambda v: v.tensor_copy(T.l0[:], T[fwn][:]), [fwn], ["l0"])
+        if r < 2:
+            S(lambda s: s.activation(T.n0[:], pick("idn", "l0"), F.Copy), ["idn", "l0"], ["n0"])
+            hop(1)
+            mates_pick()
+        for t in range(4):
+            V(lambda v: v.tensor_tensor(T.z[:, t:1024:4], pick("fa", zb, C * t), T.zg[:, C * t:C * t + C], A.add), ["fa.%d" % t, zb, "zg.%d" % t], ["z.%d" % t])
+        quant("qz", "sz", "z", ["z.%d" % t for t in range(4)])
+        if r < 2:
+            level(1)
+            mates_list(fwn)
+        else:
+            quant("qv", "sv", "vt")
+        for k in range(4):
+            op("t", lambda q: q.matmul_mx(bank(2 + k), T.wq[:, 128 * k:128 * k + 128], T.wp[:, 128 * k:128 * k + 128], T.qz[:, 0:C], T.sz[:, 0:C], True, True),
+               ["wq", "wp", "qz"], ["ps%d" % (2 + k)])
+            S(lambda s: s.activation(T.hh[:, C * k:C * k + C], bank(2 + k), F.Copy, scale=0.03125), ["ps%d" % (2 + k)], ["hh.%d" % k])
+        if r < 2:
+            hop(2)
+        xn = "x%d" % (r + 1)
+        for t in range(4):
+            V(lambda v: v.tensor_tensor(T[xn][:, t:1024:4], pick("hh", lb, C * t), T.fo[:, C * t:C * t + C], A.add), ["hh.%d" % t, lb, "fo.%d" % t], ["%s.%d" % (xn, t)])
+        quant("qx%d" % (r + 1), "sx%d" % (r + 1), xn, ["%s.%d" % (xn, t) for t in range(4)])
+        if r == 2:
+            S(lambda s: s.activation(T.nff[:], pick("idn", "l0"), F.Identity, bias=-1.0, scale=512.0), ["idn", "l0"], ["nff"])
+    op("t", lambda q: q.matmul_mx(bank(6), T.qv[:, 0:128], T.sv[:, 0:128], T.qx3[:, 0:C], T.sx3[:, 0:C], True, True), ["qv", "qx3"], ["ps6"])
+    V(lambda v: v.tensor_copy(T.yt[:], bank(6)), ["ps6"], ["yt"])
+    op("y", lambda q: q.dma_start(T.nf[:], T.nff[0:128:16, :]), ["nff"], [], "dnf", 16)
+    op("y", lambda q: q.dma_start(T.oc[:], T.qx3[:, 0:C].bitcast(U8)), ["qx3"], [], "doc", 16)
+    for k in range(4):
+        op("s", lambda q: q.dma_start(T.osc[4 * k:4 * k + 4, 0:C], T.sx3[32 * k:32 * k + 4, 0:C]), ["qx3"], [], "dos%d" % k, 16)
+    op("y", lambda q: q.dma_start(T.y[:], T.yt[:]), ["yt"], [], "dy", 16)
+    for s, n in count.items():
+        g.wait_ge(T.sem[s], n)
+    g.wait_ge(T.sem.sent, sent[0])

@@ -58,7 +58,7 @@ for _i in range(7):
 for _i in range(6):
     SCRATCH["n%d" % _i] = ("sbuf", [128, 256], "bfloat16")
     SCRATCH["l%d" % _i] = ("sbuf", [128, 16], "uint16")
-DMAS = ["dx", "dnx", "dmt", "du", "dwc", "dws", "dv", "doc", "dos0", "dos1", "dos2", "dos3", "dy", "dnf"]
+DMAS = ["dx", "dnx", "dmt", "du", "dwc", "dws", "dv", "doc", "dos0", "dos1", "dos2", "dos3", "dy0", "dy1", "dnf"]
 SEMAPHORES = ["cv", "cs", "ct", "cg", "sent"] + DMAS + ["%s%d" % (n, i) for n in ("arq", "arp", "arb") for i in range(3)]
 BIG = 1.0e29
 
@@ -75,18 +75,14 @@ def make_issue(g, T):
                 known[e][s] = n
 
     def need(e, evs):
-        todo = sorted(set(evs), key=lambda ev: -len(clock.get(ev, {})))
         best = {}
-        for sem, val in todo:
+        for sem, val in evs:
             if known[e].get(sem, 0) < val:
                 best[sem] = max(best.get(sem, 0), val)
         evs = [(sem, val) for sem, val in best.items()]
-        keep = []
         for ev in evs:
             if not any(o != ev and clock.get(o, {}).get(ev[0], 0) >= ev[1] for o in evs):
-                keep.append(ev)
-        for ev in keep:
-            queue[e].wait_ge(T.sem[ev[0]], ev[1])
+                queue[e].wait_ge(T.sem[ev[0]], ev[1])
         for ev in evs:
             learn(e, ev)
 
@@ -94,12 +90,12 @@ def make_issue(g, T):
         evs = []
         for k in reads:
             if k in writer:
-                evs.append(writer[k][0])
+                evs.append(writer[k])
             if k.startswith("ps"):
                 evs += [ev for ev, o in readers.get(k, []) if o != e]
         for k in writes:
             if k in writer:
-                evs.append(writer[k][0])
+                evs.append(writer[k])
             evs += [ev for ev, o in readers.get(k, [])]
         need(e, evs)
 
@@ -113,11 +109,11 @@ def make_issue(g, T):
         for k in reads:
             readers.setdefault(k, []).append((ev, e))
         for k in writes:
-            writer[k] = (ev, e)
+            writer[k] = ev
             readers[k] = []
 
     def lands(key, sem, val):
-        writer[key] = ((sem, val), "remote")
+        writer[key] = (sem, val)
         readers[key] = []
 
     return op, wait_for, lands, count
@@ -148,18 +144,24 @@ def rank_program(g, core, T, topo):
     def S(call, reads, writes):
         op("s", call, reads, writes)
 
-    def bank(b):
-        return T.ps[:, 512 * b:512 * b + C]
+    def both(name):
+        return [name + ".a", name + ".b"]
 
-    def mm(b, stat, stats, c0, mov, movs):
+    def bank(b, n=C):
+        return T.ps[:, 512 * b:512 * b + n]
+
+    def mm(b, stat, stats, c0, mov, movs, key=None):
         op("t", lambda q: q.matmul_mx(bank(b), T[stat][:, c0:c0 + 128], T[stats][:, c0:c0 + 128], T[mov][:, 0:C], T[movs][:, 0:C], True, True),
-           [stat, mov], ["ps%d" % b])
+           [key or stat, mov], ["ps%d" % b])
 
     def quant(q, s, tile, keys=None):
         V(lambda v: v.quantize_mx(T[q][:, :], T[s][:, :], T[tile][:, :]), keys or [tile], [q])
 
-    def pick(win, lst, a=0, n=C):
-        return T[win][:, a:a + n].indirect(T[lst][:, 0:16])
+    def pick(win, lst, a=0):
+        return T[win][:, a:a + C].indirect(T[lst][:, 0:16])
+
+    def half(win, lst, h):
+        return T[win][:, 0:C].indirect(T[lst][:, 8 * h:8 * h + 8])
 
     op("y", lambda q: q.dma_start(T.nxi[:], T.nx[:]), [], ["nxi"], "dnx", 16)
     op("s", lambda q: q.dma_start(T.x0[:], T.x[:]), [], ["x0"], "dx", 16)
@@ -170,66 +172,109 @@ def rank_program(g, core, T, topo):
     op("y", lambda q: q.dma_start(T.vt[:], T.v[:]), [], ["vt"], "dv", 16)
 
     op("g", lambda q: q.iota(T.pi[:, 0:1], [[0, 1]], 0, 1), [], ["pi"])
+    op("g", lambda q: q.iota(T.lui[:], [[16, 8]], 0, 0), [], ["lui"])
+    op("g", lambda q: q.iota(T.k16[:], [[16, 16]], 0, 0, allow_small_or_imprecise_dtypes=True), [], ["k16"])
     op("g", lambda q: q.iota(T.tj[:], [[0, 16], [1, 16]], 0, 0, allow_small_or_imprecise_dtypes=True), [], ["tj"])
     op("g", lambda q: q.iota(T.ii[:], [[1, 256]], 1, 0, allow_small_or_imprecise_dtypes=True), [], ["ii"])
-    op("g", lambda q: q.iota(T.k16[:], [[16, 16]], 0, 0, allow_small_or_imprecise_dtypes=True), [], ["k16"])
-    op("g", lambda q: q.iota(T.lui[:], [[16, 8]], 0, 0), [], ["lui"])
     V(lambda v: v.memset(T.ones[:], 1.0), [], ["ones"])
     op("g", lambda q: q.affine_select(T.et[:], T.ones[:], [[-1, 520]], A.is_equal, 0.0, 3, 4), ["ones"], ["et"])
-    for b in ("cb0", "cb1"):
-        V(lambda v: v.memset(T[b][:], 1.0), [], [b])
-    for b in ("vbz", "vb0", "vb1"):
-        V(lambda v: v.memset(T[b][:], -1.0), [], [b, b + ".0"])
-    for b in ("cb0", "cb1"):
-        V(lambda v: v.memset(T[b][:, 0:512:32], 0.0), [b], [b])
     V(lambda v: v.tensor_scalar(T.pi[:, 4:5], T.pi[:, 0:1], 15, None, A.bitwise_and), ["pi"], ["qi"])
+    V(lambda v: v.memset(T.cb0[:], 1.0), [], both("cb0"))
     V(lambda v: v.tensor_copy(T.qf[:, 0:1], T.pi[:, 4:5]), ["qi"], ["qf"])
+    V(lambda v: v.memset(T.cb1[:], 1.0), [], both("cb1"))
     V(lambda v: v.tensor_scalar(T.inv[:, 4:5], T.qf[:, 0:1], 15.0, 511.5, A.is_equal, A.mult), ["qf"], ["inv5"])
-    V(lambda v: v.tensor_scalar(T.d1[:], T.tj[:], T.qf[:, 0:1], None, A.subtract), ["tj", "qf"], ["e"])
-    V(lambda v: v.tensor_scalar(T.idn[:], T.ii[:], 1.0 / 512, None, A.mult), ["ii"], ["idn"])
+    V(lambda v: v.tensor_copy(T.lu[:], T.lui[:]), ["lui"], ["lu"])
     V(lambda v: v.tensor_scalar(T.inv[:, 0:1], T.inv[:, 4:5], 0.5, None, A.add), ["inv5"], ["inv"])
-    V(lambda v: v.tensor_scalar(T.d2[:], T.d1[:], 0.0, None, A.not_equal), ["e"], ["d2"])
     V(lambda v: v.tensor_scalar(T.cw[:], T.k16[:], T.qf[:, 0:1], None, A.add), ["k16", "qf"], ["cw"])
-    V(lambda v: v.tensor_scalar(T.ii[:], T.d1[:], 1.0, 1023.0, A.is_equal, A.mult), ["e"], ["ii"])
-    V(lambda v: v.tensor_copy(T.lid[:], T.cw[:]), ["cw"], ["lid"])
-    V(lambda v: v.tensor_tensor(T.dl[:], T.ii[:], T.d2[:], A.add), ["ii", "d2"], ["dl"])
+    V(lambda v: v.memset(T.cb0[:, 0:512:32], 0.0), both("cb0"), both("cb0"))
+    V(lambda v: v.memset(T.cb1[:, 0:512:32], 0.0), both("cb1"), both("cb1"))
+    V(lambda v: v.tensor_scalar(T.d1[:], T.tj[:], T.qf[:, 0:1], None, A.subtract), ["tj", "qf"], ["e"])
+    V(lambda v: v.tensor_copy(T.lid[:], T.cw[:]), ["cw"], both("lid"))
+    V(lambda v: v.tensor_scalar(T.d2[:], T.d1[:], 0.0, None, A.not_equal), ["e"], ["d2"])
+    V(lambda v: v.tensor_scalar(T.idn[:], T.ii[:], 1.0 / 512, None, A.mult), ["ii"], ["idn"])
     V(lambda v: v.tensor_copy(T.l0[:], T.nxi[:]), ["nxi"], ["l0"])
     S(lambda s: s.activation(T.n0[:], pick("idn", "l0"), F.Copy), ["idn", "l0"], ["n0"])
-    S(lambda s: s.activation(T.n1[:], pick("n0", "l0"), F.Copy), ["n0", "l0"], ["n1"])
-    V(lambda v: v.tensor_copy(T.fw0[:], T.nxi[:]), ["nxi"], ["fw0"])
-    V(lambda v: v.tensor_copy(T.lu[:], T.lui[:]), ["lui"], ["lu"])
+    V(lambda v: v.tensor_scalar(T.ii[:], T.d1[:], 1.0, 1023.0, A.is_equal, A.mult), ["e"], ["ii"])
     quant("qu0", "su0", "ut")
+    S(lambda s: s.activation(T.su[:, 0:128], T.su0[:, 0:128].indirect(T.lu[:, 0:8]), F.Copy), ["qu0", "lu"], ["su"])
+    S(lambda s: s.activation(T.n1[:], pick("n0", "l0"), F.Copy), ["n0", "l0"], ["n1"])
     V(lambda v: v.tensor_copy(T.qu[:, 0:128].bitcast(U32), T.qu0[:, 0:128].bitcast(U32).indirect(T.lu[:, 0:8])), ["qu0", "lu"], ["qu"])
-    V(lambda v: v.tensor_copy(T.su[:, 0:128], T.su0[:, 0:128].indirect(T.lu[:, 0:8])), ["qu0", "lu"], ["su"])
     quant("qx0", "sx0", "x0")
+    V(lambda v: v.tensor_tensor(T.dl[:], T.ii[:], T.d2[:], A.add), ["ii", "d2"], ["dl"])
 
-    def level(k):
+    def level_scan(k):
         V(lambda v: v.tensor_tensor_scan(T.nsc[:], T.dl[:], T["n%d" % k][:], 0.0, A.mult, A.max), ["dl", "n%d" % k], ["nsc"])
+
+    def level_list(k):
         V(lambda v: v.tensor_scalar(T["l%d" % k][:], T.nsc[:, 15:256:16], T.inv[:, 0:1], 1.0, A.mult, A.subtract), ["nsc", "inv"], ["l%d" % k])
 
     def hop(k):
-        out = T.n6[:] if k == 6 else T["n%d" % k][:]
+        out = T["n%d" % k][:]
         S(lambda s: s.activation(out, pick("n%d" % (k - 1), "l%d" % (k - 1)), F.Copy), ["n%d" % (k - 1), "l%d" % (k - 1)], ["n%d" % k])
 
     def mates_pick():
         S(lambda s: s.activation(T.fm[:], pick("n0", "lm"), F.Copy), ["n0", "lm"], ["fm"])
 
-    def mates_list(fw):
+    def mates_scan():
         V(lambda v: v.tensor_tensor_scan(T.fms[:], T.dl[:], T.fm[:], 0.0, A.mult, A.max), ["dl", "fm"], ["fms"])
+
+    def mates_list(fw):
         V(lambda v: v.tensor_scalar(T.fmw[:], T.fms[:, 15:256:16], T.inv[:, 0:1], 1.0, A.mult, A.subtract), ["fms", "inv"], ["fmw"])
         V(lambda v: v.tensor_tensor(T.dfm[:], T.fmw[:], T[fw][:], A.subtract), ["fmw", fw], ["dfm"])
 
-    def up(k):
-        if k == 0:
-            V(lambda v: v.tensor_copy(T.m0[:], pick("sw", "l0")), ["sw", "l0"], ["m0"])
-            return
-        win, l, other = ("sw", "l1", "m0") if k == 1 else ("m%d" % (k - 1), "l%d" % (k - 1), "mc%d" % (k % 2))
-        if k > 1:
-            S(lambda s: s.activation(T[other][:], T[win][:], F.Copy), [win], [other])
-        V(lambda v: v.tensor_tensor(T["m%d" % k][:], pick(win, l), T[other][:], A.max), [win, l, other], ["m%d" % k])
+    def up(k, halves=(0, 1)):
+        for h in halves:
+            s = [".a", ".b"][h]
+            lo, hi = 128 * h, 128 * h + 128
+            m = "m%d" % k
+            if k == 0:
+                V(lambda v: v.tensor_copy(T.m0[:, lo:hi], half("sw", "l0", h)), ["sw", "l0"], ["m0" + s])
+                continue
+            win, l, other = ("sw", "l1", "m0") if k == 1 else ("m%d" % (k - 1), "l%d" % (k - 1), "mc%d" % (k % 2))
+            V(lambda v: v.tensor_tensor(T[m][:, lo:hi], half(win, l, h), T[other][:, lo:hi], A.max),
+              ([win] if k == 1 else both(win)) + [l, other + s], [m + s])
+            if 1 <= k <= 5:
+                c = "mc%d" % ((k + 1) % 2)
+                S(lambda q: q.activation(T[c][:, lo:hi], T[m][:, lo:hi], F.Copy), [m + s], [c + s])
 
-    def unpack(b, pb, out, half):
-        S(lambda s: s.activation(T[out][:, C * b:C * b + C], bank(pb), F.Copy, scale=0.5 if half else 1.0), ["ps%d" % pb], ["%s.%d" % (out, b)])
+    def unpack(b, pb, out, factor):
+        S(lambda s: s.activation(T[out][:, C * b:C * b + C], bank(pb), F.Copy, scale=factor), ["ps%d" % pb], ["%s.%d" % (out, b)])
+
+    where = {}
+
+    def names(i):
+        vb = "vbz" if i in (0, 7) else "vb%d" % (i % 2)
+        return "cb%d" % (i % 2), "n6" if i == 0 else "nb%d" % (i % 2), "rb%d" % (i % 2), vb
+
+    def d_pick(h, i):
+        cb, nb, rb, vb = names(i)
+        s, lst, k = ".ab"[0] + "ab"[h], where[h], 6 - i if i < 7 else 0
+        lo, hi = 128 * h, 128 * h + 128
+        if i > 0:
+            S(lambda q: q.activation(T[nb][:, lo:hi], half("n%d" % k, lst, h), F.Copy), ["n%d" % k, lst + s], [nb + s])
+        lim, cmp = ("s1", A.is_gt) if i < 7 else ("s2", A.is_le)
+        V(lambda v: v.tensor_tensor(T[cb][:, 2 * lo + 1:2 * hi:2], half("m%d" % k, lst, h), T[lim][:, lo:hi], cmp), both("m%d" % k) + [lst + s, lim], [cb + s])
+
+    def d_move(h, i):
+        cb, nb, rb, vb = names(i)
+        s, lo, hi = "." + "ab"[h], 128 * h, 128 * h + 128
+        V(lambda v: v.tensor_tensor_scan(T[vb][:, 2 * lo + 1:2 * hi:2], T[nb][:, lo:hi], T[cb][:, 2 * lo + 1:2 * hi:2], 0.0, A.max, A.subtract),
+          [nb if i == 0 else nb + s, cb + s], [vb + s])
+
+    def d_keep(h, i):
+        cb, nb, rb, vb = names(i)
+        s, lo, hi = "." + "ab"[h], 256 * h, 256 * h + 256
+        V(lambda v: v.tensor_tensor_scan(T[rb][:, lo:hi], T[cb][:, lo:hi], T[vb][:, lo:hi], 0.0, A.mult, A.max), [cb + s, vb + s, vb + s + "0"], [rb + s])
+
+    def d_list(h, i, lp, lb):
+        cb, nb, rb, vb = names(i)
+        s, lo, hi = "." + "ab"[h], 256 * h, 256 * h + 256
+        out = lp if i == 6 else lb if i == 7 else "lw%d" % (i % 2)
+        V(lambda v: v.tensor_scalar(T[out][:, 8 * h:8 * h + 8], T[rb][:, lo + 31:hi:32], 512.0, -1.0, A.mult, A.add), [rb + s], [out + s])
+        where[h] = out
+        if i < 6:
+            nv = "vb%d" % ((i + 1) % 2)
+            S(lambda q: q.activation(T[nv][:, lo:hi:32], T[rb][:, lo + 31:hi:32], F.Copy), [rb + s], [nv + s + "0"])
 
     for r in range(R3):
         d = STEP[r]
@@ -245,78 +290,94 @@ def rank_program(g, core, T, topo):
         op("t", lambda q: q.matmul_mx(bank(0), T.qu[:, 0:128], T.su[:, 0:128], T[qx][:, 0:C], T[sx][:, 0:C], True, True), ["qu", "su", qx], ["ps0"])
         S(lambda s: s.activation(T.sw[:], bank(0), F.Copy), ["ps0"], ["sw"])
         if r == 0:
-            level(1)
-            hop(2)
+            level_scan(1)
             V(lambda v: v.tensor_scalar(T.mka[:], T.d2[:], -2.0 * BIG, BIG, A.mult, A.add), ["d2"], ["mka"])
-            V(lambda v: v.tensor_scalar(T.mkf[:], T.d2[:], 2.0 * BIG, -BIG, A.mult, A.add), ["d2"], ["mkf"])
-        level(2)
+            level_list(1)
+            hop(2)
+        else:
+            level_scan(2)
+            mates_scan()
+            level_list(2)
+            mates_list(fw)
+            hop(3)
         up(0)
-        hop(3)
-        if r == 0:
-            for b in range(4):
-                V(lambda v: v.quantize_mx(T.qe[:, 128 * b:128 * b + 128], T.se[:, 128 * b:128 * b + 128], T.et[:, 3 - b:515 - b]), ["et"], ["qe"])
-        V(lambda v: v.tensor_tensor(T.s1[:], T.ps[:, 0:256], T.mka[:], A.min), ["ps0", "mka"], ["s1"])
-        V(lambda v: v.tensor_tensor(T.s2[:], T.ps[:, 0:256], T.mkf[:], A.max), ["ps0", "mkf"], ["s2"])
-        for b in range(4):
-            mm(1 + b, "qe", "se", 128 * b, qx, sx)
+        V(lambda v: v.tensor_tensor(T.s1[:], bank(0), T.mka[:], A.min), ["ps0", "mka"], ["s1"])
         up(1)
-        level(3)
-        up(2)
-        hop(4)
-        level(4)
-        up(3)
-        hop(5)
-        level(5)
-        up(4)
-        hop(6)
-        up(5)
-        up(6)
         if r == 0:
-            V(lambda v: v.tensor_scalar(T.vbz[:, 0:512:32], T.cw[:], 1.0, 1.0 / 512, A.add, A.mult), ["cw"], ["vbz.0"])
-            V(lambda v: v.tensor_copy(T.mf[:], T.mti[:]), ["mti"], ["mf"])
+            level_scan(2)
+            V(lambda v: v.tensor_scalar(T.mkf[:], T.d2[:], 2.0 * BIG, -BIG, A.mult, A.add), ["d2"], ["mkf"])
+            level_list(2)
+            hop(3)
+            V(lambda v: v.memset(T.vbz[:], -1.0), [], both("vbz") + ["vbz.a0", "vbz.b0"])
             V(lambda v: v.tensor_copy(T.lm[:], T.mti[:]), ["mti"], ["lm"])
-            V(lambda v: v.tensor_tensor(T.mmin[:], T.mf[:], T.cw[:], A.min), ["mf", "cw"], ["mmin"])
-            V(lambda v: v.tensor_tensor(T.mmax[:], T.mf[:], T.cw[:], A.max), ["mf", "cw"], ["mmax"])
-            V(lambda v: v.tensor_copy(T.lmin[:], T.mmin[:]), ["mmin"], ["lmin"])
-            V(lambda v: v.tensor_copy(T.lmax[:], T.mmax[:]), ["mmax"], ["lmax"])
-            V(lambda v: v.tensor_scalar(T.dsum[:], T.tj[:], 0.0, None, A.not_equal), ["tj"], ["dsum"])
-            mates_pick()
-        now = "lid"
-        for i in range(8):
-            k = 6 - i if i < 7 else 0
-            cb, nb, rb = "cb%d" % (i % 2), "nb%d" % (i % 2), "rb%d" % (i % 2)
-            vb = "vbz" if i in (0, 7) else "vb%d" % (i % 2)
-            lst = now
-            if i == 0:
-                nb = "n6"
-            else:
-                S(lambda s: s.activation(T[nb][:], pick("n%d" % k, lst), F.Copy), ["n%d" % k, lst], [nb])
-            V(lambda v: v.tensor_tensor(T[cb][:, 1:512:2], pick("m%d" % k, lst), T.s1[:] if i < 7 else T.s2[:], A.is_gt if i < 7 else A.is_le),
-              ["m%d" % k, lst, "s1" if i < 7 else "s2"], [cb])
-            if i < 2:
-                unpack(2 * i, 1 + 2 * i, "fo", False)
-                unpack(2 * i + 1, 2 + 2 * i, "fo", False)
-                for b in ((0, 1), (2, 3))[i]:
-                    mm([5, 6, 7, 1][b], "qe", "se", 128 * b, lq, ls)
-            elif i < 4:
-                for b in (2 * i - 4, 2 * i - 3):
-                    unpack(b, [5, 6, 7, 1][b], "fa", True)
-            if i == 5 and r == 0:
-                mates_list(fw)
-            V(lambda v: v.tensor_tensor_scan(T[vb][:, 1:512:2], T[nb][:], T[cb][:, 1:512:2], 0.0, A.max, A.subtract), [nb, cb], [vb])
-            V(lambda v: v.tensor_tensor_scan(T[rb][:], T[cb][:], T[vb][:], 0.0, A.mult, A.max), [cb, vb, vb + ".0"], [rb])
-            now = lp if i == 6 else lb if i == 7 else "lw%d" % (i % 2)
-            V(lambda v: v.tensor_scalar(T[now][:], T[rb][:, 31:512:32], 512.0, -1.0, A.mult, A.add), [rb], [now])
-            if i < 6:
-                nv = "vb%d" % ((i + 1) % 2)
-                V(lambda v: v.tensor_copy(T[nv][:, 0:512:32], T[rb][:, 31:512:32]), [rb], [nv + ".0"])
-            if i == 6:
-                send(to, T[zp][:], T[lp][:], "arp%d" % r, [lp])
+            V(lambda v: v.memset(T.vb0[:], -1.0), [], both("vb0") + ["vb0.a0", "vb0.b0"])
+            V(lambda v: v.tensor_scalar(T.vbz[:, 0:512:32], T.cw[:], 1.0, 1.0 / 512, A.add, A.mult), ["cw"], ["vbz.a0", "vbz.b0"])
+        level_scan(3)
+        up(2)
+        level_list(3)
+        hop(4)
+        V(lambda v: v.tensor_tensor(T.s2[:], bank(0), T.mkf[:], A.max), ["ps0", "mkf"], ["s2"])
+        up(3)
+        level_scan(4)
+        up(4, [0])
+        level_list(4)
+        hop(5)
+        up(4, [1])
+        for b in range(4):
+            if r == 0:
+                V(lambda v: v.quantize_mx(T.qe[:, 128 * b:128 * b + 128], T.se[:, 128 * b:128 * b + 128], T.et[:, 3 - b:515 - b]), ["et"], ["qe%d" % b])
+            mm(1 + b, "qe", "se", 128 * b, qx, sx, "qe%d" % b)
+        up(5, [0])
+        level_scan(5)
+        up(5, [1])
+        if r == 0:
+            V(lambda v: v.memset(T.vb1[:], -1.0), [], both("vb1") + ["vb1.a0", "vb1.b0"])
+        level_list(5)
+        hop(6)
+        up(6)
+        where[0] = where[1] = "lid"
+        for i in range(9):
+            if i < 8:
+                d_pick(0, i)
+            if i > 0:
+                d_keep(1, i - 1)
+            if i < 8:
+                d_move(0, i)
+            if i > 0:
+                d_list(1, i - 1, lp, lb)
             if i == 7:
-                send(to, T[zb][:], T[lb][:], "arb%d" % r, [lb])
+                send(to, T[zp][:], T[lp][:], "arp%d" % r, both(lp))
+            if i == 8:
+                send(to, T[zb][:], T[lb][:], "arb%d" % r, both(lb))
+                break
+            d_keep(0, i)
+            d_pick(1, i)
+            d_list(0, i, lp, lb)
+            d_move(1, i)
+            if i < 3:
+                for b in ((0, 1), (2,), (3,))[i]:
+                    unpack(b, 1 + b, "fo", 1.0)
+            if i == 0:
+                for b in range(4):
+                    mm([5, 6, 7, 1][b], "qe", "se", 128 * b, lq, ls, "qe%d" % b)
+            if 3 <= i <= 6:
+                unpack(i - 3, [5, 6, 7, 1][i - 3], "fa", 0.5)
+            if r == 0 and i == 5:
+                mates_pick()
+                V(lambda v: v.tensor_copy(T.mf[:], T.mti[:]), ["mti"], ["mf"])
+                V(lambda v: v.tensor_copy(T.fw0[:], T.nxi[:]), ["nxi"], ["fw0"])
+                V(lambda v: v.tensor_scalar(T.dsum[:], T.tj[:], 0.0, None, A.not_equal), ["tj"], ["dsum"])
+            if r == 0 and i == 6:
+                V(lambda v: v.tensor_tensor(T.mmin[:], T.mf[:], T.cw[:], A.min), ["mf", "cw"], ["mmin"])
+                V(lambda v: v.tensor_tensor(T.mmax[:], T.mf[:], T.cw[:], A.max), ["mf", "cw"], ["mmax"])
+                mates_scan()
+            if r == 0 and i == 7:
+                V(lambda v: v.tensor_copy(T.lmin[:], T.mmin[:]), ["mmin"], ["lmin"])
+                V(lambda v: v.tensor_copy(T.lmax[:], T.mmax[:]), ["mmax"], ["lmax"])
+                mates_list(fw)
         for t in range(4):
             S(lambda s: s.activation(T.zg[:, C * t:C * t + C], pick("fa", zp, C * t), F.Copy), ["fa.%d" % t, zp], ["zg.%d" % t])
-        V(lambda v: v.tensor_copy(T.sb[:], pick("sw", lb)), ["sw", lb], ["sb"])
+        V(lambda v: v.tensor_copy(T.sb[:], pick("sw", lb)), ["sw"] + both(lb), ["sb"])
         V(lambda v: v.tensor_tensor(T.xm[:], pick("sb", "lmax"), T.mkf[:], A.max), ["sb", "lmax", "mkf"], ["xm"])
         V(lambda v: v.tensor_tensor(T.swb[:], pick("sb", "lmin"), T.xm[:], A.is_gt), ["sb", "lmin", "xm"], ["swb"])
         V(lambda v: v.tensor_tensor_scan(T.sws[:], T.dsum[:], T.swb[:], 0.0, A.mult, A.add), ["dsum", "swb"], ["sws"])
@@ -331,29 +392,36 @@ def rank_program(g, core, T, topo):
             V(lambda v: v.tensor_tensor(T.z[:, t:1024:4], pick("fa", zb, C * t), T.zg[:, C * t:C * t + C], A.add), ["fa.%d" % t, zb, "zg.%d" % t], ["z.%d" % t])
         quant("qz", "sz", "z", ["z.%d" % t for t in range(4)])
         if r < 2:
-            level(1)
-            mates_list(fwn)
+            level_scan(1)
+            level_list(1)
         else:
             quant("qv", "sv", "vt")
         for k in range(4):
             op("t", lambda q: q.matmul_mx(bank(2 + k), T.wq[:, 128 * k:128 * k + 128], T.wp[:, 128 * k:128 * k + 128], T.qz[:, 0:C], T.sz[:, 0:C], True, True),
                ["wq", "wp", "qz"], ["ps%d" % (2 + k)])
-            S(lambda s: s.activation(T.hh[:, C * k:C * k + C], bank(2 + k), F.Copy, scale=0.03125), ["ps%d" % (2 + k)], ["hh.%d" % k])
+            unpack(k, 2 + k, "hh", 0.03125)
         if r < 2:
             hop(2)
         xn = "x%d" % (r + 1)
         for t in range(4):
-            V(lambda v: v.tensor_tensor(T[xn][:, t:1024:4], pick("hh", lb, C * t), T.fo[:, C * t:C * t + C], A.add), ["hh.%d" % t, lb, "fo.%d" % t], ["%s.%d" % (xn, t)])
+            V(lambda v: v.tensor_tensor(T[xn][:, t:1024:4], pick("hh", lb, C * t), T.fo[:, C * t:C * t + C], A.add),
+              ["hh.%d" % t, "fo.%d" % t] + both(lb), ["%s.%d" % (xn, t)])
         quant("qx%d" % (r + 1), "sx%d" % (r + 1), xn, ["%s.%d" % (xn, t) for t in range(4)])
         if r == 2:
             S(lambda s: s.activation(T.nff[:], pick("idn", "l0"), F.Identity, bias=-1.0, scale=512.0), ["idn", "l0"], ["nff"])
-    op("t", lambda q: q.matmul_mx(bank(6), T.qv[:, 0:128], T.sv[:, 0:128], T.qx3[:, 0:C], T.sx3[:, 0:C], True, True), ["qv", "qx3"], ["ps6"])
-    V(lambda v: v.tensor_copy(T.yt[:], bank(6)), ["ps6"], ["yt"])
     op("y", lambda q: q.dma_start(T.nf[:], T.nff[0:128:16, :]), ["nff"], [], "dnf", 16)
     op("y", lambda q: q.dma_start(T.oc[:], T.qx3[:, 0:C].bitcast(U8)), ["qx3"], [], "doc", 16)
-    for k in range(4):
+    for h in range(2):
+        op("t", lambda q: q.matmul_mx(bank(6 + h, 128), T.qv[:, 0:128], T.sv[:, 0:128], T.qx3[:, 128 * h:128 * h + 128], T.sx3[:, 128 * h:128 * h + 128], True, True),
+           ["qv", "qx3"], ["ps%d" % (6 + h)])
+    V(lambda v: v.tensor_copy(T.yt[:, 0:128], bank(6, 128)), ["ps6"], ["yt.0"])
+    for k in range(2):
         op("s", lambda q: q.dma_start(T.osc[4 * k:4 * k + 4, 0:C], T.sx3[32 * k:32 * k + 4, 0:C]), ["qx3"], [], "dos%d" % k, 16)
-    op("y", lambda q: q.dma_start(T.y[:], T.yt[:]), ["yt"], [], "dy", 16)
+    S(lambda s: s.activation(T.yt[:, 128:256], bank(7, 128), F.Copy), ["ps7"], ["yt.1"])
+    op("y", lambda q: q.dma_start(T.y[:, 0:128], T.yt[:, 0:128]), ["yt.0"], [], "dy0", 16)
+    op("s", lambda q: q.dma_start(T.y[:, 128:256], T.yt[:, 128:256]), ["yt.1"], [], "dy1", 16)
+    for k in range(2, 4):
+        op("y", lambda q: q.dma_start(T.osc[4 * k:4 * k + 4, 0:C], T.sx3[32 * k:32 * k + 4, 0:C]), ["qx3"], [], "dos%d" % k, 16)
     for s, n in count.items():
         g.wait_ge(T.sem[s], n)
     g.wait_ge(T.sem.sent, sent[0])

@@ -21,16 +21,14 @@ SCRATCH = {
     "d1": ("sbuf", [128, 256], "float32"), "d2": ("sbuf", [128, 256], "float32"),
     "mka": ("sbuf", [128, 256], "float32"),
     "mkf": ("sbuf", [128, 256], "float32"),
-    "dl": ("sbuf", [128, 256], "bfloat16"), "dsum": ("sbuf", [128, 256], "bfloat16"),
+    "dl": ("sbuf", [128, 256], "bfloat16"),
     "lid": ("sbuf", [128, 16], "uint16"), "lu": ("sbuf", [128, 8], "uint16"), "lui": ("sbuf", [128, 8], "int32"),
     "lm": ("sbuf", [128, 16], "uint16"), "lmin": ("sbuf", [128, 16], "uint16"), "lmax": ("sbuf", [128, 16], "uint16"),
     "mf": ("sbuf", [128, 16], "float32"), "mmin": ("sbuf", [128, 16], "float32"), "mmax": ("sbuf", [128, 16], "float32"),
     "sw": ("sbuf", [128, 256], "float32"), "s1": ("sbuf", [128, 256], "float32"), "s2": ("sbuf", [128, 256], "float32"),
     "n6": ("sbuf", [128, 256], "bfloat16"), "nsc": ("sbuf", [128, 256], "bfloat16"),
-    "fm": ("sbuf", [128, 256], "bfloat16"), "fms": ("sbuf", [128, 256], "bfloat16"), "fmw": ("sbuf", [128, 16], "float32"),
-    "dfm": ("sbuf", [128, 16], "float32"), "tt": ("sbuf", [128, 16], "float32"),
+    "fm": ("sbuf", [128, 256], "bfloat16"), "fw": ("sbuf", [128, 16], "bfloat16"),
     "sb": ("sbuf", [128, 256], "float32"), "xm": ("sbuf", [128, 256], "float32"),
-    "swb": ("sbuf", [128, 256], "bfloat16"), "sws": ("sbuf", [128, 256], "bfloat16"),
     "nff": ("sbuf", [128, 256], "float32"), "yt": ("sbuf", [128, 256], "float32"),
     "fa": ("sbuf", [128, 1024], "bfloat16"), "fo": ("sbuf", [128, 1024], "bfloat16"),
     "zg": ("sbuf", [128, 1024], "bfloat16"), "z": ("sbuf", [128, 1024], "bfloat16"), "hh": ("sbuf", [128, 1024], "bfloat16"),
@@ -43,7 +41,6 @@ for _i in range(2):
         SCRATCH["%s%d" % (_n, _i)] = ("sbuf", [128, 512], "bfloat16")
     SCRATCH["nb%d" % _i] = ("sbuf", [128, 256], "bfloat16")
     SCRATCH["lw%d" % _i] = ("sbuf", [128, 16], "uint16")
-    SCRATCH["fw%d" % _i] = ("sbuf", [128, 16], "float32")
 for _i in range(4):
     SCRATCH["x%d" % _i] = ("sbuf", [128, 1024], "bfloat16")
     SCRATCH["qx%d" % _i] = ("sbuf", [128, 256], CODE)
@@ -59,7 +56,7 @@ for _i in range(6):
     SCRATCH["n%d" % _i] = ("sbuf", [128, 256], "bfloat16")
     SCRATCH["l%d" % _i] = ("sbuf", [128, 16], "uint16")
 DMAS = ["dx", "dnx", "dmt", "du", "dwc", "dws", "dv", "doc", "dos0", "dos1", "dos2", "dos3", "dy0", "dy1", "dnf"]
-SEMAPHORES = ["cv", "cs", "ct", "cg", "sent"] + DMAS + ["%s%d" % (n, i) for n in ("arq", "arp", "arb") for i in range(3)]
+SEMAPHORES = ["cv", "cs", "ct", "cg", "sent"] + DMAS + ["%s%d" % (n, i) for n in ("arq", "arp", "arb", "arc") for i in range(3)]
 BIG = 1.0e29
 
 
@@ -150,12 +147,13 @@ def rank_program(g, core, T, topo):
     def bank(b, n=C):
         return T.ps[:, 512 * b:512 * b + n]
 
-    def mm(b, stat, stats, c0, mov, movs, key=None):
-        op("t", lambda q: q.matmul_mx(bank(b), T[stat][:, c0:c0 + 128], T[stats][:, c0:c0 + 128], T[mov][:, 0:C], T[movs][:, 0:C], True, True),
-           [key or stat, mov], ["ps%d" % b])
+    def mm(b, stat, c0, mov, lo, n, reads):
+        (q, s), (x, y) = stat, mov
+        op("t", lambda e: e.matmul_mx(bank(b, n), T[q][:, c0:c0 + 128], T[s][:, c0:c0 + 128], T[x][:, lo:lo + n], T[y][:, lo:lo + n], True, True),
+           reads, ["ps%d" % b])
 
-    def quant(q, s, tile, keys=None):
-        V(lambda v: v.quantize_mx(T[q][:, :], T[s][:, :], T[tile][:, :]), keys or [tile], [q])
+    def quant(q, s, tile, key, reads, lo=0, n=128):
+        V(lambda v: v.quantize_mx(T[q][:, lo:lo + n], T[s][:, lo:lo + n], T[tile][:, 4 * lo:4 * lo + 4 * n]), reads, [key])
 
     def pick(win, lst, a=0):
         return T[win][:, a:a + C].indirect(T[lst][:, 0:16])
@@ -192,14 +190,15 @@ def rank_program(g, core, T, topo):
     V(lambda v: v.tensor_copy(T.lid[:], T.cw[:]), ["cw"], both("lid"))
     V(lambda v: v.tensor_scalar(T.d2[:], T.d1[:], 0.0, None, A.not_equal), ["e"], ["d2"])
     V(lambda v: v.tensor_scalar(T.idn[:], T.ii[:], 1.0 / 512, None, A.mult), ["ii"], ["idn"])
-    V(lambda v: v.tensor_copy(T.l0[:], T.nxi[:]), ["nxi"], ["l0"])
-    S(lambda s: s.activation(T.n0[:], pick("idn", "l0"), F.Copy), ["idn", "l0"], ["n0"])
+    V(lambda v: v.tensor_copy(T.l0[:], T.nxi[:]), ["nxi"], both("l0"))
+    S(lambda s: s.activation(T.n0[:], pick("idn", "l0"), F.Copy), ["idn"] + both("l0"), ["n0"])
     V(lambda v: v.tensor_scalar(T.ii[:], T.d1[:], 1.0, 1023.0, A.is_equal, A.mult), ["e"], ["ii"])
-    quant("qu0", "su0", "ut")
+    quant("qu0", "su0", "ut", "qu0", ["ut"])
     S(lambda s: s.activation(T.su[:, 0:128], T.su0[:, 0:128].indirect(T.lu[:, 0:8]), F.Copy), ["qu0", "lu"], ["su"])
-    S(lambda s: s.activation(T.n1[:], pick("n0", "l0"), F.Copy), ["n0", "l0"], ["n1"])
+    S(lambda s: s.activation(T.n1[:], pick("n0", "l0"), F.Copy), ["n0"] + both("l0"), ["n1"])
     V(lambda v: v.tensor_copy(T.qu[:, 0:128].bitcast(U32), T.qu0[:, 0:128].bitcast(U32).indirect(T.lu[:, 0:8])), ["qu0", "lu"], ["qu"])
-    quant("qx0", "sx0", "x0")
+    quant("qx0", "sx0", "x0", "qx0.a", ["x0"])
+    quant("qx0", "sx0", "x0", "qx0.b", ["x0"], 128)
     V(lambda v: v.tensor_tensor(T.dl[:], T.ii[:], T.d2[:], A.add), ["ii", "d2"], ["dl"])
 
     def level_scan(k):
@@ -210,17 +209,10 @@ def rank_program(g, core, T, topo):
 
     def hop(k):
         out = T["n%d" % k][:]
-        S(lambda s: s.activation(out, pick("n%d" % (k - 1), "l%d" % (k - 1)), F.Copy), ["n%d" % (k - 1), "l%d" % (k - 1)], ["n%d" % k])
+        S(lambda s: s.activation(out, pick("n%d" % (k - 1), "l%d" % (k - 1)), F.Copy), ["n%d" % (k - 1)] + (both("l0") if k == 1 else ["l%d" % (k - 1)]), ["n%d" % k])
 
     def mates_pick():
         S(lambda s: s.activation(T.fm[:], pick("n0", "lm"), F.Copy), ["n0", "lm"], ["fm"])
-
-    def mates_scan():
-        V(lambda v: v.tensor_tensor_scan(T.fms[:], T.dl[:], T.fm[:], 0.0, A.mult, A.max), ["dl", "fm"], ["fms"])
-
-    def mates_list(fw):
-        V(lambda v: v.tensor_scalar(T.fmw[:], T.fms[:, 15:256:16], T.inv[:, 0:1], 1.0, A.mult, A.subtract), ["fms", "inv"], ["fmw"])
-        V(lambda v: v.tensor_tensor(T.dfm[:], T.fmw[:], T[fw][:], A.subtract), ["fmw", fw], ["dfm"])
 
     def up(k, halves=(0, 1)):
         for h in halves:
@@ -228,17 +220,17 @@ def rank_program(g, core, T, topo):
             lo, hi = 128 * h, 128 * h + 128
             m = "m%d" % k
             if k == 0:
-                V(lambda v: v.tensor_copy(T.m0[:, lo:hi], half("sw", "l0", h)), ["sw", "l0"], ["m0" + s])
+                V(lambda v: v.tensor_copy(T.m0[:, lo:hi], half("sw", "l0", h)), both("sw") + ["l0" + s], ["m0" + s])
                 continue
             win, l, other = ("sw", "l1", "m0") if k == 1 else ("m%d" % (k - 1), "l%d" % (k - 1), "mc%d" % (k % 2))
             V(lambda v: v.tensor_tensor(T[m][:, lo:hi], half(win, l, h), T[other][:, lo:hi], A.max),
-              ([win] if k == 1 else both(win)) + [l, other + s], [m + s])
+              both(win) + [l, other + s], [m + s])
             if 1 <= k <= 5:
                 c = "mc%d" % ((k + 1) % 2)
                 S(lambda q: q.activation(T[c][:, lo:hi], T[m][:, lo:hi], F.Copy), [m + s], [c + s])
 
-    def unpack(b, pb, out, factor):
-        S(lambda s: s.activation(T[out][:, C * b:C * b + C], bank(pb), F.Copy, scale=factor), ["ps%d" % pb], ["%s.%d" % (out, b)])
+    def unpack(b, pb, out, factor, key, lo=0, n=C):
+        S(lambda s: s.activation(T[out][:, C * b + lo:C * b + lo + n], bank(pb, n), F.Copy, scale=factor), ["ps%d" % pb], [key])
 
     where = {}
 
@@ -248,12 +240,15 @@ def rank_program(g, core, T, topo):
 
     def d_pick(h, i):
         cb, nb, rb, vb = names(i)
-        s, lst, k = ".ab"[0] + "ab"[h], where[h], 6 - i if i < 7 else 0
+        s, lst, k = "." + "ab"[h], where[h], 6 - i if i < 7 else 0
         lo, hi = 128 * h, 128 * h + 128
         if i > 0:
             S(lambda q: q.activation(T[nb][:, lo:hi], half("n%d" % k, lst, h), F.Copy), ["n%d" % k, lst + s], [nb + s])
         lim, cmp = ("s1", A.is_gt) if i < 7 else ("s2", A.is_le)
-        V(lambda v: v.tensor_tensor(T[cb][:, 2 * lo + 1:2 * hi:2], half("m%d" % k, lst, h), T[lim][:, lo:hi], cmp), both("m%d" % k) + [lst + s, lim], [cb + s])
+        if i == 0:
+            V(lambda v: v.tensor_tensor(T[cb][:, 2 * lo + 1:2 * hi:2], T.m6[:, lo:hi], T.s1[:, lo:hi], A.is_gt), ["m6" + s, "s1" + s], [cb + s])
+            return
+        V(lambda v: v.tensor_tensor(T[cb][:, 2 * lo + 1:2 * hi:2], half("m%d" % k, lst, h), T[lim][:, lo:hi], cmp), both("m%d" % k) + [lst + s, lim + s], [cb + s])
 
     def d_move(h, i):
         cb, nb, rb, vb = names(i)
@@ -279,16 +274,25 @@ def rank_program(g, core, T, topo):
     for r in range(R3):
         d = STEP[r]
         to = cores[(rank + d) % len(cores)]
-        qx, sx, fw, fwn = "qx%d" % r, "sx%d" % r, "fw%d" % (r % 2), "fw%d" % ((r + 1) % 2)
+        qx, sx = "qx%d" % r, "sx%d" % r
         lq, ls, zp, zb, lp, lb = ["%s%d" % (n, r) for n in ("lq", "ls", "zp", "zb", "lp", "lb")]
         eng = len(few(cores[(rank - d) % len(cores)], core))
         lands(lq, "arq%d" % r, 2 * eng)
         lands(zp, "arp%d" % r, eng)
-        lands(zb, "arb%d" % r, eng)
-        send(to, T[lq][:, 0:C].bitcast(U8), T[qx][:, 0:C].bitcast(U8), "arq%d" % r, [qx])
-        send(to, T[ls][:, 0:C], T[sx][:, 0:C], "arq%d" % r, [qx])
-        op("t", lambda q: q.matmul_mx(bank(0), T.qu[:, 0:128], T.su[:, 0:128], T[qx][:, 0:C], T[sx][:, 0:C], True, True), ["qu", "su", qx], ["ps0"])
-        S(lambda s: s.activation(T.sw[:], bank(0), F.Copy), ["ps0"], ["sw"])
+        lands(zb + ".a", "arb%d" % r, eng)
+        lands(zb + ".b", "arc%d" % r, eng)
+        send(to, T[lq][:, 0:C].bitcast(U8), T[qx][:, 0:C].bitcast(U8), "arq%d" % r, both(qx))
+        send(to, T[ls][:, 0:C], T[sx][:, 0:C], "arq%d" % r, both(qx))
+        for h in range(2):
+            s = [".a", ".b"][h]
+            lo, hi = 128 * h, 128 * h + 128
+            mm(4 * h, ("qu", "su"), 0, (qx, sx), lo, 128, ["qu", "su", qx + s])
+            S(lambda q: q.activation(T.sw[:, lo:hi], bank(4 * h, 128), F.Copy), ["ps%d" % (4 * h)], ["sw" + s])
+
+        def limit(name, mask, f, parts):
+            for h in parts:
+                lo, hi = 128 * h, 128 * h + 128
+                V(lambda v: v.tensor_tensor(T[name][:, lo:hi], bank(4 * h, 128), T[mask][:, lo:hi], f), ["ps%d" % (4 * h), mask], [name + [".a", ".b"][h]])
         if r == 0:
             level_scan(1)
             V(lambda v: v.tensor_scalar(T.mka[:], T.d2[:], -2.0 * BIG, BIG, A.mult, A.add), ["d2"], ["mka"])
@@ -296,12 +300,9 @@ def rank_program(g, core, T, topo):
             hop(2)
         else:
             level_scan(2)
-            mates_scan()
             level_list(2)
-            mates_list(fw)
             hop(3)
         up(0)
-        V(lambda v: v.tensor_tensor(T.s1[:], bank(0), T.mka[:], A.min), ["ps0", "mka"], ["s1"])
         up(1)
         if r == 0:
             level_scan(2)
@@ -313,12 +314,14 @@ def rank_program(g, core, T, topo):
             V(lambda v: v.memset(T.vb0[:], -1.0), [], both("vb0") + ["vb0.a0", "vb0.b0"])
             V(lambda v: v.tensor_scalar(T.vbz[:, 0:512:32], T.cw[:], 1.0, 1.0 / 512, A.add, A.mult), ["cw"], ["vbz.a0", "vbz.b0"])
         level_scan(3)
+        limit("s2", "mkf", A.max, [0])
         up(2)
         level_list(3)
         hop(4)
-        V(lambda v: v.tensor_tensor(T.s2[:], bank(0), T.mkf[:], A.max), ["ps0", "mkf"], ["s2"])
+        limit("s2", "mkf", A.max, [1])
         up(3)
         level_scan(4)
+        limit("s1", "mka", A.min, [0])
         up(4, [0])
         level_list(4)
         hop(5)
@@ -326,7 +329,9 @@ def rank_program(g, core, T, topo):
         for b in range(4):
             if r == 0:
                 V(lambda v: v.quantize_mx(T.qe[:, 128 * b:128 * b + 128], T.se[:, 128 * b:128 * b + 128], T.et[:, 3 - b:515 - b]), ["et"], ["qe%d" % b])
-            mm(1 + b, "qe", "se", 128 * b, qx, sx, "qe%d" % b)
+            if b < 2:
+                mm(1 + b, ("qe", "se"), 128 * b, (qx, sx), 0, C, ["qe%d" % b] + both(qx))
+        limit("s1", "mka", A.min, [1])
         up(5, [0])
         level_scan(5)
         up(5, [1])
@@ -339,6 +344,10 @@ def rank_program(g, core, T, topo):
         for i in range(9):
             if i < 8:
                 d_pick(0, i)
+            if i == 0:
+                d_pick(1, 0)
+                unpack(0, 1, "fo", 1.0, "fo.0")
+                unpack(1, 2, "fo", 1.0, "fo.1")
             if i > 0:
                 d_keep(1, i - 1)
             if i < 8:
@@ -347,81 +356,110 @@ def rank_program(g, core, T, topo):
                 d_list(1, i - 1, lp, lb)
             if i == 7:
                 send(to, T[zp][:], T[lp][:], "arp%d" % r, both(lp))
+                S(lambda q: q.activation(T.vb0[:, 0:512:32], T.fw[:], F.Copy), ["fw"], ["vb0.a0", "vb0.b0"])
             if i == 8:
-                send(to, T[zb][:], T[lb][:], "arb%d" % r, both(lb))
+                send(to, T[zb][:, 8:16], T[lb][:, 8:16], "arc%d" % r, [lb + ".b"])
                 break
             d_keep(0, i)
-            d_pick(1, i)
+            if i > 0:
+                d_pick(1, i)
             d_list(0, i, lp, lb)
+            if i == 7:
+                send(to, T[zb][:, 0:8], T[lb][:, 0:8], "arb%d" % r, [lb + ".a"])
             d_move(1, i)
-            if i < 3:
-                for b in ((0, 1), (2,), (3,))[i]:
-                    unpack(b, 1 + b, "fo", 1.0)
             if i == 0:
                 for b in range(4):
-                    mm([5, 6, 7, 1][b], "qe", "se", 128 * b, lq, ls, "qe%d" % b)
-            if 3 <= i <= 6:
-                unpack(i - 3, [5, 6, 7, 1][i - 3], "fa", 0.5)
-            if r == 0 and i == 5:
+                    mm([6, 7, 3, 5][b], ("qe", "se"), 128 * b, (lq, ls), 0, C, ["qe%d" % b, lq])
+            if 2 <= i <= 5:
+                unpack(i - 2, [6, 7, 3, 5][i - 2], "fa", 0.5, "fa.%d" % (i - 2))
+            if i == 6:
                 mates_pick()
+            if r == 0 and i == 5:
                 V(lambda v: v.tensor_copy(T.mf[:], T.mti[:]), ["mti"], ["mf"])
-                V(lambda v: v.tensor_copy(T.fw0[:], T.nxi[:]), ["nxi"], ["fw0"])
-                V(lambda v: v.tensor_scalar(T.dsum[:], T.tj[:], 0.0, None, A.not_equal), ["tj"], ["dsum"])
+                V(lambda v: v.tensor_scalar(T.fw[:], T.nxi[:], 1.0, 1.0 / 512, A.add, A.mult), ["nxi"], ["fw"])
             if r == 0 and i == 6:
                 V(lambda v: v.tensor_tensor(T.mmin[:], T.mf[:], T.cw[:], A.min), ["mf", "cw"], ["mmin"])
                 V(lambda v: v.tensor_tensor(T.mmax[:], T.mf[:], T.cw[:], A.max), ["mf", "cw"], ["mmax"])
-                mates_scan()
             if r == 0 and i == 7:
                 V(lambda v: v.tensor_copy(T.lmin[:], T.mmin[:]), ["mmin"], ["lmin"])
                 V(lambda v: v.tensor_copy(T.lmax[:], T.mmax[:]), ["mmax"], ["lmax"])
-                mates_list(fw)
-        for t in range(4):
-            S(lambda s: s.activation(T.zg[:, C * t:C * t + C], pick("fa", zp, C * t), F.Copy), ["fa.%d" % t, zp], ["zg.%d" % t])
-        V(lambda v: v.tensor_copy(T.sb[:], pick("sw", lb)), ["sw"] + both(lb), ["sb"])
-        V(lambda v: v.tensor_tensor(T.xm[:], pick("sb", "lmax"), T.mkf[:], A.max), ["sb", "lmax", "mkf"], ["xm"])
-        V(lambda v: v.tensor_tensor(T.swb[:], pick("sb", "lmin"), T.xm[:], A.is_gt), ["sb", "lmin", "xm"], ["swb"])
-        V(lambda v: v.tensor_tensor_scan(T.sws[:], T.dsum[:], T.swb[:], 0.0, A.mult, A.add), ["dsum", "swb"], ["sws"])
-        V(lambda v: v.tensor_tensor(T.tt[:], T.sws[:, 15:256:16], T.dfm[:], A.mult), ["sws", "dfm"], ["tt"])
-        V(lambda v: v.tensor_tensor(T[fwn][:], T[fw][:], T.tt[:], A.add), [fw, "tt"], [fwn])
-        V(lambda v: v.tensor_copy(T.l0[:], T[fwn][:]), [fwn], ["l0"])
+        halves = [(0, ".a", 0, 128), (1, ".b", 128, 256)]
+        for h, s, lo, hi in halves:
+            for t in range(4):
+                S(lambda q: q.activation(T.zg[:, C * t + lo:C * t + hi], T.fa[:, C * t:C * t + C].indirect(T[zp][:, 8 * h:8 * h + 8]), F.Copy),
+                  ["fa.%d" % t, zp], ["zg.%d%s" % (t, s)])
+        for h, s, lo, hi in halves:
+            V(lambda v: v.tensor_copy(T.sb[:, lo:hi], half("sw", lb, h)), both("sw") + [lb + s], ["sb" + s])
+        for h, s, lo, hi in halves:
+            V(lambda v: v.tensor_tensor(T.xm[:, lo:hi], half("sb", "lmax", h), T.mkf[:, lo:hi], A.max), both("sb") + ["lmax", "mkf"], ["xm" + s])
+        for h, s, lo, hi in halves:
+            V(lambda v: v.tensor_tensor(T.cb0[:, 2 * lo + 1:2 * hi:2], half("sb", "lmin", h), T.xm[:, lo:hi], A.is_le), both("sb") + ["lmin", "xm" + s], ["cb0" + s])
+        for h, s, lo, hi in halves:
+            V(lambda v: v.tensor_tensor_scan(T.vb0[:, 2 * lo + 1:2 * hi:2], T.fm[:, lo:hi], T.cb0[:, 2 * lo + 1:2 * hi:2], 0.0, A.max, A.subtract), ["fm", "cb0" + s], ["vb0" + s])
+        for h, s, lo, hi in halves:
+            d_keep(h, 6)
+        for h, s, lo, hi in halves:
+            V(lambda v: v.tensor_scalar(T.l0[:, 8 * h:8 * h + 8], T.rb0[:, 2 * lo + 31:2 * hi:32], 512.0, -1.0, A.mult, A.add), ["rb0" + s], ["l0" + s])
         if r < 2:
-            S(lambda s: s.activation(T.n0[:], pick("idn", "l0"), F.Copy), ["idn", "l0"], ["n0"])
+            S(lambda q: q.activation(T.n0[:], pick("idn", "l0"), F.Copy), ["idn"] + both("l0"), ["n0"])
             hop(1)
-            mates_pick()
-        for t in range(4):
-            V(lambda v: v.tensor_tensor(T.z[:, t:1024:4], pick("fa", zb, C * t), T.zg[:, C * t:C * t + C], A.add), ["fa.%d" % t, zb, "zg.%d" % t], ["z.%d" % t])
-        quant("qz", "sz", "z", ["z.%d" % t for t in range(4)])
+            S(lambda q: q.activation(T.fw[:], T.rb0[:, 31:512:32], F.Copy), both("rb0"), ["fw"])
+        for t in (2, 3):
+            mm(4 + t, ("qe", "se"), 128 * t, (qx, sx), 0, C, ["qe%d" % t] + both(qx))
+        def z_ready(h, s, lo, hi):
+            quant("qz", "sz", "z", "qz" + s, ["z.%d%s" % (t, s) for t in range(4)], lo)
+            for k in range(4):
+                pb = [0, 1, 2, 3, 4, 5, 0, 1][k + 4 * h]
+                mm(pb, ("wq", "wp"), 128 * k, ("qz", "sz"), lo, 128, ["wq", "wp", "qz" + s])
+                unpack(k, pb, "hh", 0.03125, "hh.%d%s" % (k, s), lo, 128)
+
+        for h, s, lo, hi in halves:
+            for t in range(4):
+                V(lambda v: v.tensor_tensor(T.z[:, 4 * lo + t:4 * hi:4], T.fa[:, C * t:C * t + C].indirect(T[zb][:, 8 * h:8 * h + 8]), T.zg[:, C * t + lo:C * t + hi], A.add),
+                  ["fa.%d" % t, zb + s, "zg.%d%s" % (t, s)], ["z.%d%s" % (t, s)])
+                if h == 1 and t == 0:
+                    z_ready(*halves[0])
+        z_ready(*halves[1])
         if r < 2:
             level_scan(1)
             level_list(1)
         else:
-            quant("qv", "sv", "vt")
-        for k in range(4):
-            op("t", lambda q: q.matmul_mx(bank(2 + k), T.wq[:, 128 * k:128 * k + 128], T.wp[:, 128 * k:128 * k + 128], T.qz[:, 0:C], T.sz[:, 0:C], True, True),
-               ["wq", "wp", "qz"], ["ps%d" % (2 + k)])
-            unpack(k, 2 + k, "hh", 0.03125)
+            quant("qv", "sv", "vt", "qv", ["vt"])
+        xn = "x%d" % (r + 1)
+        def x_ready(h, s, lo, hi):
+            quant("qx%d" % (r + 1), "sx%d" % (r + 1), xn, "qx%d%s" % (r + 1, s), ["%s.%d%s" % (xn, t, s) for t in range(4)], lo)
+
+        for h, s, lo, hi in halves:
+            for t in (2, 3):
+                S(lambda q: q.activation(T.zg[:, C * t + lo:C * t + hi], T.hh[:, C * t:C * t + C].indirect(T[lb][:, 8 * h:8 * h + 8]), F.Copy),
+                  both("hh.%d" % t) + [lb + s], ["zg.%d%s" % (t, s)])
         if r < 2:
             hop(2)
-        xn = "x%d" % (r + 1)
-        for t in range(4):
-            V(lambda v: v.tensor_tensor(T[xn][:, t:1024:4], pick("hh", lb, C * t), T.fo[:, C * t:C * t + C], A.add),
-              ["hh.%d" % t, "fo.%d" % t] + both(lb), ["%s.%d" % (xn, t)])
-        quant("qx%d" % (r + 1), "sx%d" % (r + 1), xn, ["%s.%d" % (xn, t) for t in range(4)])
+        for h, s, lo, hi in halves:
+            for t in (0, 1):
+                V(lambda v: v.tensor_tensor(T[xn][:, 4 * lo + t:4 * hi:4], T.hh[:, C * t:C * t + C].indirect(T[lb][:, 8 * h:8 * h + 8]), T.fo[:, C * t + lo:C * t + hi], A.add),
+                  both("hh.%d" % t) + ["fo.%d" % t, lb + s], ["%s.%d%s" % (xn, t, s)])
+        for h, s, lo, hi in halves:
+            for t in (2, 3):
+                V(lambda v: v.tensor_tensor(T[xn][:, 4 * lo + t:4 * hi:4], T.zg[:, C * t + lo:C * t + hi], T.ps[:, 512 * (4 + t) + lo:512 * (4 + t) + hi], A.add),
+                  ["zg.%d%s" % (t, s), "ps%d" % (4 + t)], ["%s.%d%s" % (xn, t, s)])
+                if h == 1 and t == 2:
+                    x_ready(*halves[0])
+        x_ready(*halves[1])
         if r == 2:
-            S(lambda s: s.activation(T.nff[:], pick("idn", "l0"), F.Identity, bias=-1.0, scale=512.0), ["idn", "l0"], ["nff"])
+            S(lambda q: q.activation(T.nff[:], pick("idn", "l0"), F.Identity, bias=-1.0, scale=512.0), ["idn"] + both("l0"), ["nff"])
     op("y", lambda q: q.dma_start(T.nf[:], T.nff[0:128:16, :]), ["nff"], [], "dnf", 16)
-    op("y", lambda q: q.dma_start(T.oc[:], T.qx3[:, 0:C].bitcast(U8)), ["qx3"], [], "doc", 16)
+    op("y", lambda q: q.dma_start(T.oc[:], T.qx3[:, 0:C].bitcast(U8)), both("qx3"), [], "doc", 16)
     for h in range(2):
-        op("t", lambda q: q.matmul_mx(bank(6 + h, 128), T.qv[:, 0:128], T.sv[:, 0:128], T.qx3[:, 128 * h:128 * h + 128], T.sx3[:, 128 * h:128 * h + 128], True, True),
-           ["qv", "qx3"], ["ps%d" % (6 + h)])
+        mm(6 + h, ("qv", "sv"), 0, ("qx3", "sx3"), 128 * h, 128, ["qv", "qx3" + [".a", ".b"][h]])
     V(lambda v: v.tensor_copy(T.yt[:, 0:128], bank(6, 128)), ["ps6"], ["yt.0"])
     for k in range(2):
-        op("s", lambda q: q.dma_start(T.osc[4 * k:4 * k + 4, 0:C], T.sx3[32 * k:32 * k + 4, 0:C]), ["qx3"], [], "dos%d" % k, 16)
+        op("s", lambda q: q.dma_start(T.osc[4 * k:4 * k + 4, 0:C], T.sx3[32 * k:32 * k + 4, 0:C]), both("qx3"), [], "dos%d" % k, 16)
     S(lambda s: s.activation(T.yt[:, 128:256], bank(7, 128), F.Copy), ["ps7"], ["yt.1"])
     op("y", lambda q: q.dma_start(T.y[:, 0:128], T.yt[:, 0:128]), ["yt.0"], [], "dy0", 16)
     op("s", lambda q: q.dma_start(T.y[:, 128:256], T.yt[:, 128:256]), ["yt.1"], [], "dy1", 16)
     for k in range(2, 4):
-        op("y", lambda q: q.dma_start(T.osc[4 * k:4 * k + 4, 0:C], T.sx3[32 * k:32 * k + 4, 0:C]), ["qx3"], [], "dos%d" % k, 16)
+        op("y", lambda q: q.dma_start(T.osc[4 * k:4 * k + 4, 0:C], T.sx3[32 * k:32 * k + 4, 0:C]), both("qx3"), [], "dos%d" % k, 16)
     for s, n in count.items():
         g.wait_ge(T.sem[s], n)
     g.wait_ge(T.sem.sent, sent[0])

from concourse.mybir import dt, AluOpType as A, ActivationFunctionType as F

STEP = [1, 2, 4]
C = 256
R3 = 3
CODE = "float8_e4m3fn_x4"
SCRATCH = {
    "ps": ("psum", [128, 4096], "float32"),
    "ut": ("sbuf", [128, 512], "bfloat16"), "vt": ("sbuf", [128, 512], "bfloat16"),
    "qu0": ("sbuf", [128, 128], CODE), "su0": ("sbuf", [128, 128], "uint8"),
    "qu": ("sbuf", [128, 128], CODE), "su": ("sbuf", [128, 128], "uint8"),
    "qv": ("sbuf", [128, 128], CODE), "sv": ("sbuf", [128, 128], "uint8"),
    "wq": ("sbuf", [128, 512], CODE), "wp": ("sbuf", [128, 512], "uint8"),
    "ones": ("sbuf", [128, 520], "bfloat16"), "et": ("sbuf", [128, 520], "bfloat16"),
    "qe": ("sbuf", [128, 512], CODE), "se": ("sbuf", [128, 512], "uint8"),
    "nxi": ("sbuf", [128, 16], "int32"), "mti": ("sbuf", [128, 16], "int32"),
    "tj": ("sbuf", [128, 256], "float32"), "ii": ("sbuf", [128, 256], "float32"),
    "idn": ("sbuf", [128, 256], "bfloat16"),
    "pi": ("sbuf", [128, 8], "int32"), "qf": ("sbuf", [128, 8], "float32"), "inv": ("sbuf", [128, 8], "float32"),
    "k16": ("sbuf", [128, 16], "float32"), "cw": ("sbuf", [128, 16], "float32"),
    "d1": ("sbuf", [128, 256], "float32"), "d2": ("sbuf", [128, 256], "float32"),
    "mka": ("sbuf", [128, 256], "float32"),
    "mkf": ("sbuf", [128, 256], "float32"),
    "dl": ("sbuf", [128, 256], "bfloat16"),
    "lid": ("sbuf", [128, 16], "uint16"), "lu": ("sbuf", [128, 8], "uint16"), "lui": ("sbuf", [128, 8], "int32"),
    "lm": ("sbuf", [128, 16], "uint16"), "lmin": ("sbuf", [128, 16], "uint16"), "lmax": ("sbuf", [128, 16], "uint16"),
    "mf": ("sbuf", [128, 16], "float32"), "mmin": ("sbuf", [128, 16], "float32"), "mmax": ("sbuf", [128, 16], "float32"),
    "sw": ("sbuf", [128, 256], "float32"), "s1": ("sbuf", [128, 256], "float32"), "s2": ("sbuf", [128, 256], "float32"),
    "n6": ("sbuf", [128, 256], "bfloat16"), "nsc": ("sbuf", [128, 256], "bfloat16"),
    "fm": ("sbuf", [128, 256], "bfloat16"), "fw": ("sbuf", [128, 16], "bfloat16"),
    "sb": ("sbuf", [128, 256], "float32"), "xm": ("sbuf", [128, 256], "float32"),
    "nff": ("sbuf", [128, 256], "float32"), "yt": ("sbuf", [128, 256], "float32"),
    "fa": ("sbuf", [128, 1024], "bfloat16"), "fo": ("sbuf", [128, 1024], "bfloat16"),
    "zg": ("sbuf", [128, 1024], "bfloat16"), "z": ("sbuf", [128, 1024], "bfloat16"), "hh": ("sbuf", [128, 1024], "bfloat16"),
    "qz": ("sbuf", [128, 256], CODE), "sz": ("sbuf", [128, 256], "uint8"),
    "vbz": ("sbuf", [128, 512], "bfloat16"),
}
for _i in range(2):
    SCRATCH["mc%d" % _i] = ("sbuf", [128, 256], "float32")
    for _n in ("cb", "vb", "rb"):
        SCRATCH["%s%d" % (_n, _i)] = ("sbuf", [128, 512], "bfloat16")
    SCRATCH["nb%d" % _i] = ("sbuf", [128, 256], "bfloat16")
    SCRATCH["lw%d" % _i] = ("sbuf", [128, 16], "uint16")
for _i in range(4):
    SCRATCH["x%d" % _i] = ("sbuf", [128, 1024], "bfloat16")
    SCRATCH["qx%d" % _i] = ("sbuf", [128, 256], CODE)
    SCRATCH["sx%d" % _i] = ("sbuf", [128, 256], "uint8")
for _i in range(3):
    SCRATCH["lq%d" % _i] = ("sbuf", [128, 256], CODE)
    SCRATCH["ls%d" % _i] = ("sbuf", [128, 256], "uint8")
    for _n in ("lp", "lb", "zp", "zb"):
        SCRATCH["%s%d" % (_n, _i)] = ("sbuf", [128, 16], "uint16")
for _i in range(7):
    SCRATCH["m%d" % _i] = ("sbuf", [128, 256], "float32")
for _i in range(6):
    SCRATCH["n%d" % _i] = ("sbuf", [128, 256], "bfloat16")
    SCRATCH["l%d" % _i] = ("sbuf", [128, 16], "uint16")
DMAS = ["dx", "dnx", "dmt", "du", "dwc", "dws", "dv", "doc", "dos0", "dos1", "dos2", "dos3", "dy0", "dy1", "dnf"]
SEMAPHORES = ["cv", "cs", "ct", "cg", "sent"] + DMAS + ["%s%d" % (n, i) for n in ("arq", "arp", "arb", "arc") for i in range(3)]
BIG = 1.0e29


def make_issue(g, T):
    queue = {"v": g.vector, "s": g.scalar, "t": g.tensor, "g": g, "y": g.sync}
    known = {e: {} for e in queue}
    count, clock, writer, readers = {}, {}, {}, {}

    def learn(e, ev):
        sem, val = ev
        for s, n in list(clock.get(ev, {}).items()) + [(sem, val)]:
            if known[e].get(s, 0) < n:
                known[e][s] = n

    def need(e, evs):
        best = {}
        for sem, val in evs:
            if known[e].get(sem, 0) < val:
                best[sem] = max(best.get(sem, 0), val)
        evs = [(sem, val) for sem, val in best.items()]
        for ev in evs:
            if not any(o != ev and clock.get(o, {}).get(ev[0], 0) >= ev[1] for o in evs):
                queue[e].wait_ge(T.sem[ev[0]], ev[1])
        for ev in evs:
            learn(e, ev)

    def wait_for(e, reads=(), writes=()):
        evs = []
        for k in reads:
            if k in writer:
                evs.append(writer[k])
            if k.startswith("ps"):
                evs += [ev for ev, o in readers.get(k, []) if o != e]
        for k in writes:
            if k in writer:
                evs.append(writer[k])
            evs += [ev for ev, o in readers.get(k, [])]
        need(e, evs)

    def op(e, call, reads=(), writes=(), sem=None, inc=1):
        wait_for(e, reads, writes)
        sem = sem or "c" + e
        call(queue[e]).then_inc(T.sem[sem], inc)
        count[sem] = count.get(sem, 0) + inc
        ev = (sem, count[sem])
        clock[ev] = dict(known[e])
        for k in reads:
            readers.setdefault(k, []).append((ev, e))
        for k in writes:
            writer[k] = ev
            readers[k] = []

    def lands(key, sem, val):
        writer[key] = (sem, val)
        readers[key] = []

    return op, wait_for, lands, count


def rank_program(g, core, T, topo):
    rank = T.rank_of(core)
    if rank is None:
        return
    op, wait_for, lands, count = make_issue(g, T)
    cores = T.cores
    U8, U32 = dt.uint8, dt.uint32
    sent = [0]

    def few(src, dst):
        return topo.engines(src, dst)[:8]

    def send(dst, out, src, sem, reads):
        wait_for("g", reads)
        rid, pid = topo.addr(dst)[:2]
        e = few(core, dst)
        g.remote_dma(out, src, T.sem[sem], T.sem.sent, pid, rid, sum(1 << k for k in e))
        sent[0] += len(e)

    def V(call, reads, writes):
        op("v", call, reads, writes)

    def S(call, reads, writes):
        op("s", call, reads, writes)

    def both(name):
        return [name + ".a", name + ".b"]

    def bank(b, n=C):
        return T.ps[:, 512 * b:512 * b + n]

    def mm(b, stat, c0, mov, lo, n, reads):
        (q, s), (x, y) = stat, mov
        op("t", lambda e: e.matmul_mx(bank(b, n), T[q][:, c0:c0 + 128], T[s][:, c0:c0 + 128], T[x][:, lo:lo + n], T[y][:, lo:lo + n], True, True),
           reads, ["ps%d" % b])

    def quant(q, s, tile, key, reads, lo=0, n=128):
        V(lambda v: v.quantize_mx(T[q][:, lo:lo + n], T[s][:, lo:lo + n], T[tile][:, 4 * lo:4 * lo + 4 * n]), reads, [key])

    def pick(win, lst, a=0):
        return T[win][:, a:a + C].indirect(T[lst][:, 0:16])

    def half(win, lst, h):
        return T[win][:, 0:C].indirect(T[lst][:, 8 * h:8 * h + 8])

    op("y", lambda q: q.dma_start(T.nxi[:], T.nx[:]), [], ["nxi"], "dnx", 16)
    op("s", lambda q: q.dma_start(T.x0[:], T.x[:]), [], ["x0"], "dx", 16)
    op("y", lambda q: q.dma_start(T.ut[:], T.u[:]), [], ["ut"], "du", 16)
    op("y", lambda q: q.dma_start(T.mti[:], T.mt[:]), [], ["mti"], "dmt", 16)
    op("y", lambda q: q.dma_start(T.wq[:, 0:512].bitcast(U8), T.wc[:]), [], ["wq"], "dwc", 16)
    op("y", lambda q: q.dma_start(T.wp[:, 0:512], T.ws[:]), [], ["wp"], "dws", 16)
    op("y", lambda q: q.dma_start(T.vt[:], T.v[:]), [], ["vt"], "dv", 16)

    op("g", lambda q: q.iota(T.pi[:, 0:1], [[0, 1]], 0, 1), [], ["pi"])
    op("g", lambda q: q.iota(T.lui[:], [[16, 8]], 0, 0), [], ["lui"])
    op("g", lambda q: q.iota(T.k16[:], [[16, 16]], 0, 0, allow_small_or_imprecise_dtypes=True), [], ["k16"])
    op("g", lambda q: q.iota(T.tj[:], [[0, 16], [1, 16]], 0, 0, allow_small_or_imprecise_dtypes=True), [], ["tj"])
    op("g", lambda q: q.iota(T.ii[:], [[1, 256]], 1, 0, allow_small_or_imprecise_dtypes=True), [], ["ii"])
    V(lambda v: v.memset(T.ones[:], 1.0), [], ["ones"])
    op("g", lambda q: q.affine_select(T.et[:], T.ones[:], [[-1, 520]], A.is_equal, 0.0, 3, 4), ["ones"], ["et"])
    V(lambda v: v.tensor_scalar(T.pi[:, 4:5], T.pi[:, 0:1], 15, None, A.bitwise_and), ["pi"], ["qi"])
    V(lambda v: v.memset(T.cb0[:], 1.0), [], both("cb0"))
    V(lambda v: v.tensor_copy(T.qf[:, 0:1], T.pi[:, 4:5]), ["qi"], ["qf"])
    V(lambda v: v.memset(T.cb1[:], 1.0), [], both("cb1"))
    V(lambda v: v.tensor_scalar(T.inv[:, 4:5], T.qf[:, 0:1], 15.0, 511.5, A.is_equal, A.mult), ["qf"], ["inv5"])
    V(lambda v: v.tensor_copy(T.lu[:], T.lui[:]), ["lui"], ["lu"])
    V(lambda v: v.tensor_scalar(T.inv[:, 0:1], T.inv[:, 4:5], 0.5, None, A.add), ["inv5"], ["inv"])
    V(lambda v: v.tensor_scalar(T.cw[:], T.k16[:], T.qf[:, 0:1], None, A.add), ["k16", "qf"], ["cw"])
    V(lambda v: v.memset(T.cb0[:, 0:512:32], 0.0), both("cb0"), both("cb0"))
    V(lambda v: v.memset(T.cb1[:, 0:512:32], 0.0), both("cb1"), both("cb1"))
    V(lambda v: v.tensor_scalar(T.d1[:], T.tj[:], T.qf[:, 0:1], None, A.subtract), ["tj", "qf"], ["e"])
    V(lambda v: v.tensor_copy(T.lid[:], T.cw[:]), ["cw"], both("lid"))
    V(lambda v: v.tensor_scalar(T.d2[:], T.d1[:], 0.0, None, A.not_equal), ["e"], ["d2"])
    V(lambda v: v.tensor_scalar(T.idn[:], T.ii[:], 1.0 / 512, None, A.mult), ["ii"], ["idn"])
    V(lambda v: v.tensor_copy(T.l0[:], T.nxi[:]), ["nxi"], both("l0"))
    S(lambda s: s.activation(T.n0[:], pick("idn", "l0"), F.Copy), ["idn"] + both("l0"), ["n0"])
    V(lambda v: v.tensor_scalar(T.ii[:], T.d1[:], 1.0, 1023.0, A.is_equal, A.mult), ["e"], ["ii"])
    quant("qu0", "su0", "ut", "qu0", ["ut"])
    S(lambda s: s.activation(T.su[:, 0:128], T.su0[:, 0:128].indirect(T.lu[:, 0:8]), F.Copy), ["qu0", "lu"], ["su"])
    S(lambda s: s.activation(T.n1[:], pick("n0", "l0"), F.Copy), ["n0"] + both("l0"), ["n1"])
    V(lambda v: v.tensor_copy(T.qu[:, 0:128].bitcast(U32), T.qu0[:, 0:128].bitcast(U32).indirect(T.lu[:, 0:8])), ["qu0", "lu"], ["qu"])
    quant("qx0", "sx0", "x0", "qx0.a", ["x0"])
    quant("qx0", "sx0", "x0", "qx0.b", ["x0"], 128)
    V(lambda v: v.tensor_tensor(T.dl[:], T.ii[:], T.d2[:], A.add), ["ii", "d2"], ["dl"])

    def level_scan(k):
        V(lambda v: v.tensor_tensor_scan(T.nsc[:], T.dl[:], T["n%d" % k][:], 0.0, A.mult, A.max), ["dl", "n%d" % k], ["nsc"])

    def level_list(k):
        V(lambda v: v.tensor_scalar(T["l%d" % k][:], T.nsc[:, 15:256:16], T.inv[:, 0:1], 1.0, A.mult, A.subtract), ["nsc", "inv"], ["l%d" % k])

    def hop(k):
        out = T["n%d" % k][:]
        S(lambda s: s.activation(out, pick("n%d" % (k - 1), "l%d" % (k - 1)), F.Copy), ["n%d" % (k - 1)] + (both("l0") if k == 1 else ["l%d" % (k - 1)]), ["n%d" % k])

    def mates_pick():
        S(lambda s: s.activation(T.fm[:], pick("n0", "lm"), F.Copy), ["n0", "lm"], ["fm"])

    def up(k, halves=(0, 1)):
        for h in halves:
            s = [".a", ".b"][h]
            lo, hi = 128 * h, 128 * h + 128
            m = "m%d" % k
            if k == 0:
                V(lambda v: v.tensor_copy(T.m0[:, lo:hi], half("sw", "l0", h)), both("sw") + ["l0" + s], ["m0" + s])
                continue
            win, l, other = ("sw", "l1", "m0") if k == 1 else ("m%d" % (k - 1), "l%d" % (k - 1), "mc%d" % (k % 2))
            V(lambda v: v.tensor_tensor(T[m][:, lo:hi], half(win, l, h), T[other][:, lo:hi], A.max),
              both(win) + [l, other + s], [m + s])
            if 1 <= k <= 5:
                c = "mc%d" % ((k + 1) % 2)
                S(lambda q: q.activation(T[c][:, lo:hi], T[m][:, lo:hi], F.Copy), [m + s], [c + s])

    def unpack(b, pb, out, factor, key, lo=0, n=C):
        S(lambda s: s.activation(T[out][:, C * b + lo:C * b + lo + n], bank(pb, n), F.Copy, scale=factor), ["ps%d" % pb], [key])

    where = {}

    def names(i):
        vb = "vbz" if i in (0, 7) else "vb%d" % (i % 2)
        return "cb%d" % (i % 2), "n6" if i == 0 else "nb%d" % (i % 2), "rb%d" % (i % 2), vb

    def d_pick(h, i):
        cb, nb, rb, vb = names(i)
        s, lst, k = "." + "ab"[h], where[h], 6 - i if i < 7 else 0
        lo, hi = 128 * h, 128 * h + 128
        if i > 0:
            S(lambda q: q.activation(T[nb][:, lo:hi], half("n%d" % k, lst, h), F.Copy), ["n%d" % k, lst + s], [nb + s])
        lim, cmp = ("s1", A.is_gt) if i < 7 else ("s2", A.is_le)
        if i == 0:
            V(lambda v: v.tensor_tensor(T[cb][:, 2 * lo + 1:2 * hi:2], T.m6[:, lo:hi], T.s1[:, lo:hi], A.is_gt), ["m6" + s, "s1" + s], [cb + s])
            return
        V(lambda v: v.tensor_tensor(T[cb][:, 2 * lo + 1:2 * hi:2], half("m%d" % k, lst, h), T[lim][:, lo:hi], cmp), both("m%d" % k) + [lst + s, lim + s], [cb + s])

    def d_move(h, i):
        cb, nb, rb, vb = names(i)
        s, lo, hi = "." + "ab"[h], 128 * h, 128 * h + 128
        V(lambda v: v.tensor_tensor_scan(T[vb][:, 2 * lo + 1:2 * hi:2], T[nb][:, lo:hi], T[cb][:, 2 * lo + 1:2 * hi:2], 0.0, A.max, A.subtract),
          [nb if i == 0 else nb + s, cb + s], [vb + s])

    def d_keep(h, i):
        cb, nb, rb, vb = names(i)
        s, lo, hi = "." + "ab"[h], 256 * h, 256 * h + 256
        V(lambda v: v.tensor_tensor_scan(T[rb][:, lo:hi], T[cb][:, lo:hi], T[vb][:, lo:hi], 0.0, A.mult, A.max), [cb + s, vb + s, vb + s + "0"], [rb + s])

    def d_list(h, i, lp, lb):
        cb, nb, rb, vb = names(i)
        s, lo, hi = "." + "ab"[h], 256 * h, 256 * h + 256
        out = lp if i == 6 else lb if i == 7 else "lw%d" % (i % 2)
        V(lambda v: v.tensor_scalar(T[out][:, 8 * h:8 * h + 8], T[rb][:, lo + 31:hi:32], 512.0, -1.0, A.mult, A.add), [rb + s], [out + s])
        where[h] = out
        if i < 6:
            nv = "vb%d" % ((i + 1) % 2)
            S(lambda q: q.activation(T[nv][:, lo:hi:32], T[rb][:, lo + 31:hi:32], F.Copy), [rb + s], [nv + s + "0"])

    for r in range(R3):
        d = STEP[r]
        to = cores[(rank + d) % len(cores)]
        qx, sx = "qx%d" % r, "sx%d" % r
        lq, ls, zp, zb, lp, lb = ["%s%d" % (n, r) for n in ("lq", "ls", "zp", "zb", "lp", "lb")]
        eng = len(few(cores[(rank - d) % len(cores)], core))
        lands(lq, "arq%d" % r, 2 * eng)
        lands(zp, "arp%d" % r, eng)
        lands(zb + ".a", "arb%d" % r, eng)
        lands(zb + ".b", "arc%d" % r, eng)
        send(to, T[lq][:, 0:C].bitcast(U8), T[qx][:, 0:C].bitcast(U8), "arq%d" % r, both(qx))
        send(to, T[ls][:, 0:C], T[sx][:, 0:C], "arq%d" % r, both(qx))
        for h in range(2):
            s = [".a", ".b"][h]
            lo, hi = 128 * h, 128 * h + 128
            mm(4 * h, ("qu", "su"), 0, (qx, sx), lo, 128, ["qu", "su", qx + s])
            S(lambda q: q.activation(T.sw[:, lo:hi], bank(4 * h, 128), F.Copy), ["ps%d" % (4 * h)], ["sw" + s])

        def limit(name, mask, f, parts):
            for h in parts:
                lo, hi = 128 * h, 128 * h + 128
                V(lambda v: v.tensor_tensor(T[name][:, lo:hi], bank(4 * h, 128), T[mask][:, lo:hi], f), ["ps%d" % (4 * h), mask], [name + [".a", ".b"][h]])
        if r == 0:
            level_scan(1)
            V(lambda v: v.tensor_scalar(T.mka[:], T.d2[:], -2.0 * BIG, BIG, A.mult, A.add), ["d2"], ["mka"])
            level_list(1)
            hop(2)
        else:
            level_scan(2)
            level_list(2)
            hop(3)
        up(0)
        up(1)
        if r == 0:
            level_scan(2)
            V(lambda v: v.tensor_scalar(T.mkf[:], T.d2[:], 2.0 * BIG, -BIG, A.mult, A.add), ["d2"], ["mkf"])
            level_list(2)
            hop(3)
            V(lambda v: v.memset(T.vbz[:], -1.0), [], both("vbz") + ["vbz.a0", "vbz.b0"])
            V(lambda v: v.tensor_copy(T.lm[:], T.mti[:]), ["mti"], ["lm"])
            V(lambda v: v.memset(T.vb0[:], -1.0), [], both("vb0") + ["vb0.a0", "vb0.b0"])
            V(lambda v: v.tensor_scalar(T.vbz[:, 0:512:32], T.cw[:], 1.0, 1.0 / 512, A.add, A.mult), ["cw"], ["vbz.a0", "vbz.b0"])
        level_scan(3)
        limit("s2", "mkf", A.max, [0])
        up(2)
        level_list(3)
        hop(4)
        limit("s2", "mkf", A.max, [1])
        up(3)
        level_scan(4)
        limit("s1", "mka", A.min, [0])
        up(4, [0])
        level_list(4)
        hop(5)
        up(4, [1])
        for b in range(4):
            if r == 0:
                V(lambda v: v.quantize_mx(T.qe[:, 128 * b:128 * b + 128], T.se[:, 128 * b:128 * b + 128], T.et[:, 3 - b:515 - b]), ["et"], ["qe%d" % b])
            if b < 2:
                mm(1 + b, ("qe", "se"), 128 * b, (qx, sx), 0, C, ["qe%d" % b] + both(qx))
        limit("s1", "mka", A.min, [1])
        up(5, [0])
        level_scan(5)
        up(5, [1])
        if r == 0:
            V(lambda v: v.memset(T.vb1[:], -1.0), [], both("vb1") + ["vb1.a0", "vb1.b0"])
        level_list(5)
        hop(6)
        up(6)
        where[0] = where[1] = "lid"
        for i in range(9):
            if i < 8:
                d_pick(0, i)
            if i == 0:
                d_pick(1, 0)
                unpack(0, 1, "fo", 1.0, "fo.0")
                unpack(1, 2, "fo", 1.0, "fo.1")
            if i > 0:
                d_keep(1, i - 1)
            if i < 8:
                d_move(0, i)
            if i > 0:
                d_list(1, i - 1, lp, lb)
            if i == 7:
                send(to, T[zp][:], T[lp][:], "arp%d" % r, both(lp))
                S(lambda q: q.activation(T.vb0[:, 0:512:32], T.fw[:], F.Copy), ["fw"], ["vb0.a0", "vb0.b0"])
            if i == 8:
                send(to, T[zb][:, 8:16], T[lb][:, 8:16], "arc%d" % r, [lb + ".b"])
                break
            d_keep(0, i)
            if i > 0:
                d_pick(1, i)
            d_list(0, i, lp, lb)
            if i == 7:
                send(to, T[zb][:, 0:8], T[lb][:, 0:8], "arb%d" % r, [lb + ".a"])
            d_move(1, i)
            if i == 0:
                for b in range(4):
                    mm([6, 7, 3, 5][b], ("qe", "se"), 128 * b, (lq, ls), 0, C, ["qe%d" % b, lq])
            if 2 <= i <= 5:
                unpack(i - 2, [6, 7, 3, 5][i - 2], "fa", 0.5, "fa.%d" % (i - 2))
            if i == 6:
                mates_pick()
            if r == 0 and i == 5:
                V(lambda v: v.tensor_copy(T.mf[:], T.mti[:]), ["mti"], ["mf"])
                V(lambda v: v.tensor_scalar(T.fw[:], T.nxi[:], 1.0, 1.0 / 512, A.add, A.mult), ["nxi"], ["fw"])
            if r == 0 and i == 6:
                V(lambda v: v.tensor_tensor(T.mmin[:], T.mf[:], T.cw[:], A.min), ["mf", "cw"], ["mmin"])
                V(lambda v: v.tensor_tensor(T.mmax[:], T.mf[:], T.cw[:], A.max), ["mf", "cw"], ["mmax"])
            if r == 0 and i == 7:
                V(lambda v: v.tensor_copy(T.lmin[:], T.mmin[:]), ["mmin"], ["lmin"])
                V(lambda v: v.tensor_copy(T.lmax[:], T.mmax[:]), ["mmax"], ["lmax"])
        halves = [(0, ".a", 0, 128), (1, ".b", 128, 256)]
        for h, s, lo, hi in halves:
            for t in range(4):
                S(lambda q: q.activation(T.zg[:, C * t + lo:C * t + hi], T.fa[:, C * t:C * t + C].indirect(T[zp][:, 8 * h:8 * h + 8]), F.Copy),
                  ["fa.%d" % t, zp], ["zg.%d%s" % (t, s)])
        for h, s, lo, hi in halves:
            V(lambda v: v.tensor_copy(T.sb[:, lo:hi], half("sw", lb, h)), both("sw") + [lb + s], ["sb" + s])
        for h, s, lo, hi in halves:
            V(lambda v: v.tensor_tensor(T.xm[:, lo:hi], half("sb", "lmax", h), T.mkf[:, lo:hi], A.max), both("sb") + ["lmax", "mkf"], ["xm" + s])
        for h, s, lo, hi in halves:
            V(lambda v: v.tensor_tensor(T.cb0[:, 2 * lo + 1:2 * hi:2], half("sb", "lmin", h), T.xm[:, lo:hi], A.is_le), both("sb") + ["lmin", "xm" + s], ["cb0" + s])
        for h, s, lo, hi in halves:
            V(lambda v: v.tensor_tensor_scan(T.vb0[:, 2 * lo + 1:2 * hi:2], T.fm[:, lo:hi], T.cb0[:, 2 * lo + 1:2 * hi:2], 0.0, A.max, A.subtract), ["fm", "cb0" + s], ["vb0" + s])
        for h, s, lo, hi in halves:
            d_keep(h, 6)
        for h, s, lo, hi in halves:
            V(lambda v: v.tensor_scalar(T.l0[:, 8 * h:8 * h + 8], T.rb0[:, 2 * lo + 31:2 * hi:32], 512.0, -1.0, A.mult, A.add), ["rb0" + s], ["l0" + s])
        if r < 2:
            S(lambda q: q.activation(T.n0[:], pick("idn", "l0"), F.Copy), ["idn"] + both("l0"), ["n0"])
            hop(1)
            S(lambda q: q.activation(T.fw[:], T.rb0[:, 31:512:32], F.Copy), both("rb0"), ["fw"])
        for t in (2, 3):
            mm(4 + t, ("qe", "se"), 128 * t, (qx, sx), 0, C, ["qe%d" % t] + both(qx))
        def z_ready(h, s, lo, hi):
            quant("qz", "sz", "z", "qz" + s, ["z.%d%s" % (t, s) for t in range(4)], lo)
            for k in range(4):
                pb = [0, 1, 2, 3, 4, 5, 0, 1][k + 4 * h]
                mm(pb, ("wq", "wp"), 128 * k, ("qz", "sz"), lo, 128, ["wq", "wp", "qz" + s])
                unpack(k, pb, "hh", 0.03125, "hh.%d%s" % (k, s), lo, 128)

        for h, s, lo, hi in halves:
            for t in range(4):
                V(lambda v: v.tensor_tensor(T.z[:, 4 * lo + t:4 * hi:4], T.fa[:, C * t:C * t + C].indirect(T[zb][:, 8 * h:8 * h + 8]), T.zg[:, C * t + lo:C * t + hi], A.add),
                  ["fa.%d" % t, zb + s, "zg.%d%s" % (t, s)], ["z.%d%s" % (t, s)])
                if h == 1 and t == 0:
                    z_ready(*halves[0])
        z_ready(*halves[1])
        if r < 2:
            level_scan(1)
            level_list(1)
        else:
            quant("qv", "sv", "vt", "qv", ["vt"])
        xn = "x%d" % (r + 1)
        def x_ready(h, s, lo, hi):
            quant("qx%d" % (r + 1), "sx%d" % (r + 1), xn, "qx%d%s" % (r + 1, s), ["%s.%d%s" % (xn, t, s) for t in range(4)], lo)

        for h, s, lo, hi in halves:
            for t in (2, 3):
                S(lambda q: q.activation(T.zg[:, C * t + lo:C * t + hi], T.hh[:, C * t:C * t + C].indirect(T[lb][:, 8 * h:8 * h + 8]), F.Copy),
                  both("hh.%d" % t) + [lb + s], ["zg.%d%s" % (t, s)])
        if r < 2:
            hop(2)
        for h, s, lo, hi in halves:
            for t in (0, 1):
                V(lambda v: v.tensor_tensor(T[xn][:, 4 * lo + t:4 * hi:4], T.hh[:, C * t:C * t + C].indirect(T[lb][:, 8 * h:8 * h + 8]), T.fo[:, C * t + lo:C * t + hi], A.add),
                  both("hh.%d" % t) + ["fo.%d" % t, lb + s], ["%s.%d%s" % (xn, t, s)])
        for h, s, lo, hi in halves:
            for t in (2, 3):
                V(lambda v: v.tensor_tensor(T[xn][:, 4 * lo + t:4 * hi:4], T.zg[:, C * t + lo:C * t + hi], T.ps[:, 512 * (4 + t) + lo:512 * (4 + t) + hi], A.add),
                  ["zg.%d%s" % (t, s), "ps%d" % (4 + t)], ["%s.%d%s" % (xn, t, s)])
                if h == 1 and t == 2:
                    x_ready(*halves[0])
        x_ready(*halves[1])
        if r == 2:
            S(lambda q: q.activation(T.nff[:], pick("idn", "l0"), F.Identity, bias=-1.0, scale=512.0), ["idn"] + both("l0"), ["nff"])
    op("y", lambda q: q.dma_start(T.nf[:], T.nff[0:128:16, :]), ["nff"], [], "dnf", 16)
    op("y", lambda q: q.dma_start(T.oc[:], T.qx3[:, 0:C].bitcast(U8)), both("qx3"), [], "doc", 16)
    for h in range(2):
        mm(6 + h, ("qv", "sv"), 0, ("qx3", "sx3"), 128 * h, 128, ["qv", "qx3" + [".a", ".b"][h]])
    V(lambda v: v.tensor_copy(T.yt[:, 0:128], bank(6, 128)), ["ps6"], ["yt.0"])
    for k in range(2):
        op("s", lambda q: q.dma_start(T.osc[4 * k:4 * k + 4, 0:C], T.sx3[32 * k:32 * k + 4, 0:C]), both("qx3"), [], "dos%d" % k, 16)
    S(lambda s: s.activation(T.yt[:, 128:256], bank(7, 128), F.Copy), ["ps7"], ["yt.1"])
    op("y", lambda q: q.dma_start(T.y[:, 0:128], T.yt[:, 0:128]), ["yt.0"], [], "dy0", 16)
    op("s", lambda q: q.dma_start(T.y[:, 128:256], T.yt[:, 128:256]), ["yt.1"], [], "dy1", 16)
    for k in range(2, 4):
        op("y", lambda q: q.dma_start(T.osc[4 * k:4 * k + 4, 0:C], T.sx3[32 * k:32 * k + 4, 0:C]), both("qx3"), [], "dos%d" % k, 16)
    for s, n in count.items():
        g.wait_ge(T.sem[s], n)
    g.wait_ge(T.sem.sent, sent[0])
